import numpy as np
import ml_dtypes


def mxq(x, axis, fmt="e4m3"):
    dtype, down = {"e4m3": (ml_dtypes.float8_e4m3fn, 7), "e5m2": (ml_dtypes.float8_e5m2, 14)}[fmt]
    v = np.moveaxis(np.asarray(x, np.float32).astype(ml_dtypes.bfloat16).astype(np.float64), axis, -1)
    blocks = v.reshape(v.shape[:-1] + (-1, 32))
    amax = np.abs(blocks).max(-1, keepdims=True)
    byte = np.maximum(np.where(amax > 0, np.frexp(amax)[1] - 1 + 127, 0) - down, 1)
    scale = np.exp2(byte - 127.0)
    codes = (blocks / scale).astype(np.float32).astype(dtype).astype(np.float64)
    return np.moveaxis((codes * scale).reshape(v.shape), -1, axis)


WIDE = False


def mx_kscale(k):
    if not WIDE:
        return np.ones(k)
    levels = np.array([10, -10, 5, -5, 0])
    if k % 512:
        return np.exp2(np.random.permutation(np.resize(levels, k // 32))).repeat(32)
    a = np.empty((k // 512, 16))
    for p in range(k // 512):
        a[p, :8] = np.random.permutation(np.resize(levels, 8))
        for g in range(8):
            far = levels[np.abs(levels - a[p, g]) >= 10]
            a[p, g + 8] = far[np.random.randint(len(far))]
    return np.exp2(a.ravel()).repeat(32)


def f64(x):
    return np.asarray(x).astype(np.float64)


E2M1 = np.array([0.0, 0.5, 1.0, 1.5, 2.0, 3.0, 4.0, 6.0, -0.0, -0.5, -1.0, -1.5, -2.0, -3.0, -4.0, -6.0])


def pack_weight(w, fmt):
    k, n = w.shape
    w = f64(np.asarray(w, np.float32).astype(ml_dtypes.bfloat16)).reshape(k // 32, 32, n)
    amax = np.abs(w).max(1)
    if fmt == "e4m3":
        byte = np.frexp(amax)[1] - 1 + 127 - 7
    else:
        mant, ex = np.frexp(amax / 6.0)
        byte = np.where(mant > 0.5, ex, ex - 1) + 127
    byte = np.clip(np.where(amax > 0, byte, 1), 1, 254)
    scaled = (w * np.exp2(127.0 - byte)[:, None, :]).reshape(k, n).astype(np.float32)
    by_word = np.ascontiguousarray(scaled.reshape(k // 512, 128, 4, n).transpose(0, 1, 3, 2))
    if fmt == "e4m3":
        words = by_word.astype(ml_dtypes.float8_e4m3fn).view(np.uint8)
    else:
        c = by_word.astype(ml_dtypes.float4_e2m1fn).view(np.uint8) & 0xF
        words = (c[..., 0::2] | (c[..., 1::2] << 4)).reshape(k // 512, 128, 2 * n)
    return np.ascontiguousarray(words), np.ascontiguousarray(byte.astype(np.uint8).reshape(k // 512, 16, n))


def unpack_weight(words, scales, fmt):
    g, _, n = scales.shape
    words = np.ascontiguousarray(words).reshape(g, 128, n, -1)
    if fmt == "e4m3":
        vals = words.view(ml_dtypes.float8_e4m3fn).astype(np.float64)
    else:
        nib = np.empty((g, 128, n, 4), np.uint8)
        nib[..., 0::2] = words & 0xF
        nib[..., 1::2] = words >> 4
        vals = E2M1[nib]
    vals = vals * np.repeat(np.exp2(scales.astype(np.float64) - 127.0), 8, axis=1)[..., None]
    return vals.transpose(0, 1, 3, 2).reshape(g * 512, n)


def planes(y):
    n, m = y.shape
    v = y.astype(np.float32).astype(ml_dtypes.bfloat16).astype(np.float64).reshape(n // 32, 32, m)
    top = np.abs(v).max(1)
    byte = np.clip(np.where(top > 0, np.frexp(top)[1] - 1 + 127 - 7, 1), 1, 254)
    codes = (v * np.exp2(127.0 - byte)[:, None, :]).reshape(n, m).astype(np.float32).astype(ml_dtypes.float8_e4m3fn).view(np.uint8)
    words = codes.reshape(n // 512, 128, 4, m).transpose(0, 1, 3, 2)
    return np.ascontiguousarray(words), np.ascontiguousarray(byte.astype(np.uint8).reshape(n // 512, 16, m))


K, M, T = 512, 1536, 512


def setup_inputs():
    n = np.random.standard_normal
    s = mx_kscale(K)[:, None]
    u = mx_kscale(T)[:, None]
    q = n((K, T)) * s
    p_vc = pack_weight(0.1 * n((T, M)) / u, "e2m1")
    return {
        "qc": (q).astype(np.float32),
        "kc": (n((K, T)) / np.sqrt(K) / s).astype(np.float32),
        "qd": (q * 0.995 ** (np.arange(T) + 1.0)).astype(np.float32),
        "st": (n((K, M)) / np.sqrt(K) / s).astype(np.float32),
        "vc_words": p_vc[0],
        "vc_scales": p_vc[1],
        "dm": (np.tril(0.995 ** (np.arange(T)[:, None] - np.arange(T)[None])).T * u).astype(np.float32),
    }


def reference(qc, kc, qd, st, vc_words, vc_scales, dm):
    qc_ = mxq(f64(qc), 0, "e4m3")
    kc_ = mxq(f64(kc), 0, "e4m3")
    qd_ = mxq(f64(qd), 0, "e4m3")
    st_ = mxq(f64(st), 0, "e4m3")
    vc_ = unpack_weight(vc_words, vc_scales, "e2m1")
    h_ = mxq((kc_.T @ qc_) * f64(dm), 0, "e4m3")
    y = vc_.T @ h_ + st_.T @ qd_
    out_0 = np.maximum(y, 0.0) ** 2
    return (out_0,) + planes(out_0)

@@ -1,0 +1,294 @@
+from contextlib import ExitStack
+
+import concourse.mybir as mybir
+
+K, M, T = 512, 1536, 512
+FLOPS = 2 * K * T * T + 2 * T * M * T + 2 * K * M * T
+
+F32 = mybir.dt.float32
+BF16 = mybir.dt.bfloat16
+U32 = mybir.dt.uint32
+I32 = mybir.dt.int32
+U8 = mybir.dt.uint8
+FP8X4 = mybir.dt.float8_e4m3fn_x4
+FP4X4 = mybir.dt.float4_e2m1fn_x4
+ACT = mybir.ActivationFunctionType
+ALU = mybir.AluOpType
+
+P = 128
+PACK = 4
+GROUP = P * PACK
+GROUPS = M // GROUP
+HALF = T // 2
+
+
+def tile_mix_linattn_fm_pl_relu2_kernel(tc, qc, kc, qd, st, vc_words, vc_scales, dm, out_0, out_1, out_2):
+    nc = tc.nc
+    with ExitStack() as ctx:
+        sb = ctx.enter_context(tc.tile_pool(name="sb", bufs=1))
+        psum = ctx.enter_context(tc.psum_pool(name="psum", bufs=1))
+        ctx.enter_context(tc.manual_schedule())
+
+        def tile(name, shape, dtype):
+            return sb.tile(shape, dtype, name=name, align_bytes=64)
+
+        def bank(number, name):
+            return psum.tile([P, T], F32, name=name, tag="bank%d" % number)
+
+        vcw_raw = tile("vcw_raw", [P, 2 * M], U8)
+        vcs_raw = tile("vcs_raw", [P, M], U8)
+        vcw = tile("vcw", [P, 2 * M], U8)
+        vcs = tile("vcs", [P, M], U8)
+        kc_raw = tile("kc_raw", [P, PACK, T], F32)
+        qc_raw = tile("qc_raw", [P, PACK, T], F32)
+        dm_raw = tile("dm_raw", [P, PACK, T], F32)
+        qd_raw = [tile("qd_raw%d" % h, [P, PACK, HALF], F32) for h in range(2)]
+        st0_raw = [tile("st0_raw%d" % h, [P, PACK, HALF], F32) for h in range(2)]
+        st_raw = [None] + [tile("st_raw%d" % a, [P, PACK, GROUP], F32) for a in range(1, GROUPS)]
+        names = ["kc", "qc", "qd", "h"] + ["st%d" % a for a in range(GROUPS)] + ["o%d" % a for a in range(GROUPS)]
+        grouped = {n: tile(n + "_bf", [P, PACK * T], BF16) for n in names}
+        codes = {n: tile(n + "_codes", [P, T], U32) for n in names}
+        scales = {n: tile(n + "_scales", [P, T], U8) for n in names[:7]}
+        out_scales = tile("out_scales", [P, GROUPS, T], U8)
+        relu = [tile("relu%d" % a, [P, PACK, T], F32) for a in range(GROUPS)]
+        result = [tile("result%d" % a, [P, PACK, T], F32) for a in range(GROUPS)]
+        warm = tile("warm", [P, 8], F32)
+        hbank = {}
+        ybank = {}
+
+        def rows4(ap):
+            return ap.rearrange("(p j) w -> p j w", j=PACK)
+
+        nc.vector.memset(vcs_raw[:].bitcast(I32), 0)
+        nc.vector.memset(warm[:], 0.0)
+        nc.sync.dma_start(out=vcw_raw[:].bitcast(I32), in_=vc_words[0].bitcast(I32))
+        for q in range(4):
+            nc.scalar.dma_start(out=vcs_raw[32 * q : 32 * q + 4, :].bitcast(I32), in_=vc_scales[0, 4 * q : 4 * q + 4, :].bitcast(I32))
+        nc.scalar.activation(out=warm[:], in_=warm[:], func=ACT.Relu)
+        nc.sync.dma_start(out=kc_raw[:], in_=rows4(kc))
+        nc.sync.dma_start(out=qc_raw[:], in_=rows4(qc))
+        nc.sync.dma_start(out=dm_raw[:], in_=rows4(dm))
+        for h in range(2):
+            nc.sync.dma_start(out=st0_raw[h][:], in_=rows4(st[:, h * HALF : (h + 1) * HALF]))
+        for h in range(2):
+            nc.sync.dma_start(out=qd_raw[h][:], in_=rows4(qd[:, h * HALF : (h + 1) * HALF]))
+        for a in range(1, GROUPS):
+            nc.sync.dma_start(out=st_raw[a][:], in_=rows4(st[:, a * GROUP : (a + 1) * GROUP]))
+
+        def copy(engine, out, in_):
+            if engine == "V":
+                nc.vector.tensor_copy(out=out, in_=in_)
+            else:
+                nc.scalar.copy(out=out, in_=in_)
+
+        def deal_words(a):
+            src = vcw_raw[:, 2 * GROUP * a : 2 * GROUP * (a + 1)].rearrange("p (m r b) -> p r m b", r=PACK, b=2)
+            dst = vcw[:, 2 * GROUP * a : 2 * GROUP * (a + 1)].rearrange("p (r m b) -> p r m b", r=PACK, b=2)
+            nc.vector.tensor_copy(out=dst, in_=src)
+
+        def deal_scales():
+            src = vcs_raw[:].rearrange("p (a m r) -> p r a m", a=GROUPS, r=PACK)
+            dst = vcs[:].rearrange("p (a r m) -> p r a m", a=GROUPS, r=PACK)
+            nc.vector.tensor_copy(out=dst, in_=src)
+
+        def cast_dealt(engine, name, raw, raw_m0, m0, m1):
+            src = raw[:, :, PACK * (m0 - raw_m0) : PACK * (m1 - raw_m0)].rearrange("p j (m r) -> p m j r", r=PACK)
+            dst = grouped[name][:].rearrange("p (r m j) -> p m j r", r=PACK, j=PACK)[:, m0:m1]
+            copy(engine, dst, src)
+
+        def cast_plain(engine, name, raw, raw_c0, c0, c1):
+            src = raw[:, :, c0 - raw_c0 : c1 - raw_c0].rearrange("p j (c i) -> p c j i", i=PACK)
+            dst = grouped[name][:, PACK * c0 : PACK * c1].rearrange("p (c i j) -> p c j i", i=PACK, j=PACK)
+            copy(engine, dst, src)
+
+        def quant(name, c0, c1, plane=None):
+            if plane is None:
+                plane = scales[name][:, c0:c1]
+            nc.vector.quantize_mx(out=codes[name][:, c0:c1].bitcast(FP8X4), scales=plane, in_=grouped[name][:, PACK * c0 : PACK * c1])
+
+        def h_matmuls(tb):
+            hbank[tb] = bank(tb, "hbank%d" % tb)
+            cols = slice(tb * P, (tb + 1) * P)
+            for i in range(PACK):
+                keys = slice(i * P, (i + 1) * P)
+                nc.tensor.matmul_mx(
+                    out=hbank[tb][:, keys],
+                    lhsT=codes["kc"][:, keys].bitcast(FP8X4),
+                    lhsT_scale=scales["kc"][:, keys],
+                    rhs=codes["qc"][:, cols].bitcast(FP8X4),
+                    rhs_scale=scales["qc"][:, cols],
+                    start=True,
+                    stop=True,
+                )
+
+        def h_decay(tb):
+            nc.vector.tensor_tensor(
+                out=grouped["h"][:, GROUP * tb : GROUP * (tb + 1)].rearrange("p (t i) -> p t i", i=PACK),
+                in0=hbank[tb][:].rearrange("p (i t) -> p t i", i=PACK),
+                in1=dm_raw[:, :, tb * P : (tb + 1) * P].rearrange("p i t -> p t i"),
+                op=ALU.mult,
+            )
+
+        def y_values(a, r):
+            ybank[a, r] = bank((PACK * (a + 1) + r) % 8, "ybank%d_%d" % (a, r))
+            col = a * GROUP + r * P
+            nc.tensor.matmul_mx(
+                out=ybank[a, r][:],
+                lhsT=vcw[:, 2 * col : 2 * (col + P)].bitcast(FP4X4),
+                lhsT_scale=vcs[:, col : col + P],
+                rhs=codes["h"][:].bitcast(FP8X4),
+                rhs_scale=scales["h"][:],
+                start=True,
+                stop=False,
+            )
+
+        def y_state(a, r):
+            name = "st%d" % a
+            cols = slice(r * P, (r + 1) * P)
+            nc.tensor.matmul_mx(
+                out=ybank[a, r][:],
+                lhsT=codes[name][:, cols].bitcast(FP8X4),
+                lhsT_scale=scales[name][:, cols],
+                rhs=codes["qd"][:].bitcast(FP8X4),
+                rhs_scale=scales["qd"][:],
+                start=False,
+                stop=True,
+            )
+
+        def step_relu(engine, a, r, c0=0, c1=T):
+            if engine == "V":
+                nc.vector.tensor_scalar(out=relu[a][:, r, c0:c1], in0=ybank[a, r][:, c0:c1], scalar1=0.0, scalar2=None, op0=ALU.max)
+            else:
+                nc.scalar.activation(out=relu[a][:, r, c0:c1], in_=ybank[a, r][:, c0:c1], func=ACT.Relu)
+
+        def step_square(engine, a, r0, r1, c0=0, c1=T):
+            if engine == "V":
+                nc.vector.tensor_tensor(out=result[a][:, r0:r1, c0:c1], in0=relu[a][:, r0:r1, c0:c1], in1=relu[a][:, r0:r1, c0:c1], op=ALU.mult)
+            else:
+                nc.scalar.activation(out=result[a][:, r0:r1, c0:c1], in_=relu[a][:, r0:r1, c0:c1], func=ACT.Square)
+
+        def store_result(a, r0, r1, c0=0, c1=T):
+            nc.sync.dma_start(out=rows4(out_0[a * GROUP : (a + 1) * GROUP, :])[:, r0:r1, c0:c1], in_=result[a][:, r0:r1, c0:c1])
+
+        def out_cast(a, c0, c1):
+            cast_plain("V", "o%d" % a, result[a], 0, c0, c1)
+
+        def out_quant(a, c0, c1):
+            quant("o%d" % a, c0, c1, out_scales[:, a, c0:c1])
+
+        def store_words(a, c0, c1):
+            nc.sync.dma_start(
+                out=out_1[a].rearrange("p t i -> p (t i)")[:, PACK * c0 : PACK * c1].bitcast(I32),
+                in_=codes["o%d" % a][:, c0:c1].bitcast(I32),
+            )
+
+        def store_scales(q, queue):
+            queue.dma_start(
+                out=out_2.rearrange("a q t -> q a t")[4 * q : 4 * q + 4].bitcast(I32),
+                in_=out_scales[32 * q : 32 * q + 4].bitcast(I32),
+            )
+
+        deal_words(0)
+        deal_scales()
+        deal_words(1)
+        cast_dealt("V", "kc", kc_raw, 0, 0, 32)
+        cast_dealt("S", "kc", kc_raw, 0, 96, 128)
+        cast_dealt("V", "kc", kc_raw, 0, 32, 64)
+        cast_dealt("V", "kc", kc_raw, 0, 64, 96)
+        quant("kc", 0, T)
+        cast_plain("S", "qc", qc_raw, 0, 256, 384)
+        cast_plain("V", "qc", qc_raw, 0, 0, 128)
+        cast_plain("V", "qc", qc_raw, 0, 128, 256)
+        cast_plain("S", "qc", qc_raw, 0, 384, 512)
+        quant("qc", 0, 256)
+        h_matmuls(0)
+        h_matmuls(1)
+        quant("qc", 256, 512)
+        deal_words(2)
+        h_matmuls(2)
+        h_matmuls(3)
+        h_decay(0)
+        h_decay(1)
+        cast_dealt("S", "st0", st0_raw[0], 0, 0, 64)
+        h_decay(2)
+        h_decay(3)
+        cast_dealt("S", "st0", st0_raw[1], 64, 64, 128)
+        quant("h", 0, T)
+        y_values(0, 0)
+        y_values(0, 1)
+        y_values(0, 2)
+        y_values(0, 3)
+        y_values(1, 0)
+        y_values(1, 1)
+        y_values(1, 2)
+        y_values(1, 3)
+        cast_plain("S", "qd", qd_raw[0], 0, 0, 128)
+        quant("st0", 0, T)
+        cast_plain("V", "qd", qd_raw[0], 0, 128, 256)
+        cast_plain("S", "qd", qd_raw[1], 256, 256, 384)
+        cast_plain("V", "qd", qd_raw[1], 256, 384, 512)
+        quant("qd", 0, 256)
+        quant("qd", 256, 512)
+        y_state(0, 0)
+        y_state(0, 1)
+        y_state(0, 2)
+        y_state(0, 3)
+        step_relu("S", 0, 0)
+        cast_dealt("V", "st1", st_raw[1], 0, 0, 64)
+        step_relu("S", 0, 1)
+        cast_dealt("V", "st1", st_raw[1], 0, 64, 128)
+        step_relu("S", 0, 2)
+        step_relu("S", 0, 3)
+        y_values(2, 0)
+        y_values(2, 1)
+        quant("st1", 0, T)
+        step_square("S", 0, 0, 2)
+        store_result(0, 0, 2)
+        y_values(2, 2)
+        y_values(2, 3)
+        cast_dealt("V", "st2", st_raw[2], 0, 0, 64)
+        y_state(1, 0)
+        y_state(1, 1)
+        y_state(1, 2)
+        y_state(1, 3)
+        cast_dealt("V", "st2", st_raw[2], 0, 64, 128)
+        step_square("S", 0, 2, 4)
+        store_result(0, 2, 4)
+        step_relu("V", 1, 0)
+        step_relu("S", 1, 1)
+        quant("st2", 0, T)
+        step_relu("S", 1, 2)
+        cast_plain("V", "o0", result[0], 0, 0, 256)
+        y_state(2, 0)
+        y_state(2, 1)
+        y_state(2, 2)
+        y_state(2, 3)
+        step_relu("S", 1, 3)
+        step_square("V", 1, 0, 2)
+        store_result(1, 0, 2)
+        step_relu("S", 2, 0)
+        step_relu("S", 2, 1)
+        step_square("V", 1, 2, 4)
+        store_result(1, 2, 4)
+        step_relu("S", 2, 2)
+        step_relu("S", 2, 3)
+        cast_plain("V", "o0", result[0], 0, 256, 512)
+        step_square("S", 2, 0, 4, 0, 256)
+        out_quant(0, 0, 256)
+        out_quant(0, 256, 512)
+        store_words(0, 0, T)
+        store_result(2, 0, 4, 0, 256)
+        cast_plain("V", "o1", result[1], 0, 0, 256)
+        step_square("S", 2, 0, 4, 256, 512)
+        store_result(2, 0, 4, 256, 512)
+        cast_plain("V", "o1", result[1], 0, 256, 512)
+        out_quant(1, 0, 256)
+        cast_plain("S", "o2", result[2], 0, 0, 256)
+        out_quant(1, 256, 512)
+        store_words(1, 0, T)
+        cast_plain("V", "o2", result[2], 0, 256, 512)
+        out_quant(2, 0, 256)
+        out_quant(2, 256, 512)
+        store_words(2, 0, T)
+        for q in range(4):
+            store_scales(q, nc.scalar if q % 2 else nc.sync)

@@ -63,7 +63,7 @@ def tile_mix_linattn_fm_pl_relu2_kernel(tc, qc, kc, qd, st, vc_words, vc_scales,
         nc.vector.memset(warm[:], 0.0)
         nc.sync.dma_start(out=vcw_raw[:].bitcast(I32), in_=vc_words[0].bitcast(I32))
         for q in range(4):
-            nc.scalar.dma_start(out=vcs_raw[32 * q : 32 * q + 4, :].bitcast(I32), in_=vc_scales[0, 4 * q : 4 * q + 4, :].bitcast(I32))
+            nc.sync.dma_start(out=vcs_raw[32 * q : 32 * q + 4, :].bitcast(I32), in_=vc_scales[0, 4 * q : 4 * q + 4, :].bitcast(I32))
         nc.scalar.activation(out=warm[:], in_=warm[:], func=ACT.Relu)
         nc.sync.dma_start(out=kc_raw[:], in_=rows4(kc))
         nc.sync.dma_start(out=qc_raw[:], in_=rows4(qc))

@@ -42,9 +42,8 @@ def tile_mix_linattn_fm_pl_relu2_kernel(tc, qc, kc, qd, st, vc_words, vc_scales,
         kc_raw = tile("kc_raw", [P, PACK, T], F32)
         qc_raw = tile("qc_raw", [P, PACK, T], F32)
         dm_raw = tile("dm_raw", [P, PACK, T], F32)
-        qd_raw = [tile("qd_raw%d" % h, [P, PACK, HALF], F32) for h in range(2)]
-        st0_raw = [tile("st0_raw%d" % h, [P, PACK, HALF], F32) for h in range(2)]
-        st_raw = [None] + [tile("st_raw%d" % a, [P, PACK, GROUP], F32) for a in range(1, GROUPS)]
+        qd_raw = tile("qd_raw", [P, PACK, T], F32)
+        st_raw = [tile("st_raw%d" % a, [P, PACK, GROUP], F32) for a in range(GROUPS)]
         names = ["kc", "qc", "qd", "h"] + ["st%d" % a for a in range(GROUPS)] + ["o%d" % a for a in range(GROUPS)]
         grouped = {n: tile(n + "_bf", [P, PACK * T], BF16) for n in names}
         codes = {n: tile(n + "_codes", [P, T], U32) for n in names}
@@ -62,16 +61,14 @@ def tile_mix_linattn_fm_pl_relu2_kernel(tc, qc, kc, qd, st, vc_words, vc_scales,
         nc.vector.memset(vcs_raw[:].bitcast(I32), 0)
         nc.vector.memset(warm[:], 0.0)
         nc.sync.dma_start(out=vcw_raw[:].bitcast(I32), in_=vc_words[0].bitcast(I32))
+        nc.sync.dma_start(out=kc_raw[:], in_=rows4(kc))
         for q in range(4):
             nc.sync.dma_start(out=vcs_raw[32 * q : 32 * q + 4, :].bitcast(I32), in_=vc_scales[0, 4 * q : 4 * q + 4, :].bitcast(I32))
         nc.scalar.activation(out=warm[:], in_=warm[:], func=ACT.Relu)
-        nc.sync.dma_start(out=kc_raw[:], in_=rows4(kc))
         nc.sync.dma_start(out=qc_raw[:], in_=rows4(qc))
         nc.sync.dma_start(out=dm_raw[:], in_=rows4(dm))
-        for h in range(2):
-            nc.sync.dma_start(out=st0_raw[h][:], in_=rows4(st[:, h * HALF : (h + 1) * HALF]))
-        for h in range(2):
-            nc.sync.dma_start(out=qd_raw[h][:], in_=rows4(qd[:, h * HALF : (h + 1) * HALF]))
+        nc.sync.dma_start(out=st_raw[0][:], in_=rows4(st[:, 0:GROUP]))
+        nc.sync.dma_start(out=qd_raw[:], in_=rows4(qd))
         for a in range(1, GROUPS):
             nc.sync.dma_start(out=st_raw[a][:], in_=rows4(st[:, a * GROUP : (a + 1) * GROUP]))
 
@@ -92,8 +89,8 @@ def tile_mix_linattn_fm_pl_relu2_kernel(tc, qc, kc, qd, st, vc_words, vc_scales,
             nc.vector.tensor_copy(out=dst, in_=src)
 
         def cast_dealt(engine, name, raw, raw_m0, m0, m1):
-            src = raw[:, :, PACK * (m0 - raw_m0) : PACK * (m1 - raw_m0)].rearrange("p j (m r) -> p m j r", r=PACK)
-            dst = grouped[name][:].rearrange("p (r m j) -> p m j r", r=PACK, j=PACK)[:, m0:m1]
+            src = raw[:, :, PACK * (m0 - raw_m0) : PACK * (m1 - raw_m0)].rearrange("p j (m r) -> p m r j", r=PACK)
+            dst = grouped[name][:].rearrange("p (r m j) -> p m r j", r=PACK, j=PACK)[:, m0:m1]
             copy(engine, dst, src)
 
         def cast_plain(engine, name, raw, raw_c0, c0, c1):
@@ -188,107 +185,89 @@ def tile_mix_linattn_fm_pl_relu2_kernel(tc, qc, kc, qd, st, vc_words, vc_scales,
                 in_=out_scales[32 * q : 32 * q + 4].bitcast(I32),
             )
 
-        deal_words(0)
+        for a in range(GROUPS):
+            deal_words(a)
+        cast_dealt("S", "kc", kc_raw, 0, 16, P)
+        cast_dealt("V", "kc", kc_raw, 0, 0, 16)
         deal_scales()
-        deal_words(1)
-        cast_dealt("V", "kc", kc_raw, 0, 0, 32)
-        cast_dealt("S", "kc", kc_raw, 0, 96, 128)
-        cast_dealt("V", "kc", kc_raw, 0, 32, 64)
-        cast_dealt("V", "kc", kc_raw, 0, 64, 96)
+        cast_plain("S", "qc", qc_raw, 0, 128, HALF)
+        cast_plain("S", "qc", qc_raw, 0, HALF, T)
         quant("kc", 0, T)
-        cast_plain("S", "qc", qc_raw, 0, 256, 384)
         cast_plain("V", "qc", qc_raw, 0, 0, 128)
-        cast_plain("V", "qc", qc_raw, 0, 128, 256)
-        cast_plain("S", "qc", qc_raw, 0, 384, 512)
-        quant("qc", 0, 256)
+        quant("qc", 0, HALF)
         h_matmuls(0)
         h_matmuls(1)
-        quant("qc", 256, 512)
-        deal_words(2)
+        quant("qc", HALF, T)
         h_matmuls(2)
         h_matmuls(3)
-        h_decay(0)
-        h_decay(1)
-        cast_dealt("S", "st0", st0_raw[0], 0, 0, 64)
-        h_decay(2)
-        h_decay(3)
-        cast_dealt("S", "st0", st0_raw[1], 64, 64, 128)
+        for tb in range(4):
+            h_decay(tb)
+        cast_dealt("S", "st0", st_raw[0], 0, 48, P)
+        cast_dealt("V", "st0", st_raw[0], 0, 0, 48)
         quant("h", 0, T)
-        y_values(0, 0)
-        y_values(0, 1)
-        y_values(0, 2)
-        y_values(0, 3)
+        for r in range(PACK):
+            y_values(0, r)
         y_values(1, 0)
         y_values(1, 1)
+        quant("st0", 0, T)
+        cast_plain("S", "qd", qd_raw, 0, 384, T)
+        cast_plain("V", "qd", qd_raw, 0, HALF, 384)
+        cast_plain("V", "qd", qd_raw, 0, 0, HALF)
+        quant("qd", HALF, T)
+        quant("qd", 0, HALF)
+        for r in range(PACK):
+            y_state(0, r)
         y_values(1, 2)
         y_values(1, 3)
-        cast_plain("S", "qd", qd_raw[0], 0, 0, 128)
-        quant("st0", 0, T)
-        cast_plain("V", "qd", qd_raw[0], 0, 128, 256)
-        cast_plain("S", "qd", qd_raw[1], 256, 256, 384)
-        cast_plain("V", "qd", qd_raw[1], 256, 384, 512)
-        quant("qd", 0, 256)
-        quant("qd", 256, 512)
-        y_state(0, 0)
-        y_state(0, 1)
-        y_state(0, 2)
-        y_state(0, 3)
+        cast_dealt("V", "st1", st_raw[1], 0, 0, P)
         step_relu("S", 0, 0)
-        cast_dealt("V", "st1", st_raw[1], 0, 0, 64)
         step_relu("S", 0, 1)
-        cast_dealt("V", "st1", st_raw[1], 0, 64, 128)
         step_relu("S", 0, 2)
-        step_relu("S", 0, 3)
-        y_values(2, 0)
-        y_values(2, 1)
-        quant("st1", 0, T)
+        step_relu("V", 0, 3)
+        for r in range(3):
+            y_values(2, r)
         step_square("S", 0, 0, 2)
         store_result(0, 0, 2)
-        y_values(2, 2)
+        quant("st1", 0, T)
+        for r in range(PACK):
+            y_state(1, r)
         y_values(2, 3)
-        cast_dealt("V", "st2", st_raw[2], 0, 0, 64)
-        y_state(1, 0)
-        y_state(1, 1)
-        y_state(1, 2)
-        y_state(1, 3)
-        cast_dealt("V", "st2", st_raw[2], 0, 64, 128)
+        cast_dealt("V", "st2", st_raw[2], 0, 0, P)
         step_square("S", 0, 2, 4)
         store_result(0, 2, 4)
-        step_relu("V", 1, 0)
-        step_relu("S", 1, 1)
+        cast_plain("V", "o0", result[0], 0, 0, HALF)
         quant("st2", 0, T)
+        for r in range(PACK):
+            y_state(2, r)
+        step_relu("S", 1, 0)
+        step_relu("S", 1, 1)
         step_relu("S", 1, 2)
-        cast_plain("V", "o0", result[0], 0, 0, 256)
-        y_state(2, 0)
-        y_state(2, 1)
-        y_state(2, 2)
-        y_state(2, 3)
-        step_relu("S", 1, 3)
-        step_square("V", 1, 0, 2)
+        step_relu("V", 1, 3)
+        step_square("S", 1, 0, 2)
         store_result(1, 0, 2)
-        step_relu("S", 2, 0)
-        step_relu("S", 2, 1)
+        cast_plain("V", "o0", result[0], 0, HALF, T)
+        out_quant(0, 0, HALF)
+        out_quant(0, HALF, T)
+        store_words(0, 0, T)
         step_square("V", 1, 2, 4)
         store_result(1, 2, 4)
+        step_relu("S", 2, 0)
+        step_relu("S", 2, 1)
         step_relu("S", 2, 2)
-        step_relu("S", 2, 3)
-        cast_plain("V", "o0", result[0], 0, 256, 512)
-        step_square("S", 2, 0, 4, 0, 256)
-        out_quant(0, 0, 256)
-        out_quant(0, 256, 512)
-        store_words(0, 0, T)
-        store_result(2, 0, 4, 0, 256)
-        cast_plain("V", "o1", result[1], 0, 0, 256)
-        step_square("S", 2, 0, 4, 256, 512)
-        store_result(2, 0, 4, 256, 512)
-        cast_plain("V", "o1", result[1], 0, 256, 512)
-        out_quant(1, 0, 256)
-        cast_plain("S", "o2", result[2], 0, 0, 256)
-        out_quant(1, 256, 512)
+        step_relu("V", 2, 3)
+        step_square("S", 2, 0, 2)
+        store_result(2, 0, 2)
+        cast_plain("V", "o1", result[1], 0, 0, HALF)
+        cast_plain("V", "o1", result[1], 0, HALF, T)
+        step_square("S", 2, 2, 4)
+        store_result(2, 2, 4)
+        out_quant(1, 0, HALF)
+        cast_plain("S", "o2", result[2], 0, HALF, T)
+        cast_plain("V", "o2", result[2], 0, 0, HALF)
+        out_quant(1, HALF, T)
         store_words(1, 0, T)
-        cast_plain("V", "o2", result[2], 0, 256, 512)
-        out_quant(2, 0, 256)
-        out_quant(2, 256, 512)
+        out_quant(2, 0, HALF)
+        out_quant(2, HALF, T)
         store_words(2, 0, T)
         for q in range(4):
             store_scales(q, nc.scalar if q % 2 else nc.sync)

@@ -19,11 +19,15 @@ P = 128
 PACK = 4
 GROUP = P * PACK
 GROUPS = M // GROUP
-HALF = T // 2
+BANKS = 8
+QUADRANT = 32
+QUARTER, HALF = T // 4, T // 2
+LAST_SPLIT = 320
 
 
 def tile_mix_linattn_fm_pl_relu2_kernel(tc, qc, kc, qd, st, vc_words, vc_scales, dm, out_0, out_1, out_2):
     nc = tc.nc
+    vector, scalar = nc.vector.tensor_copy, nc.scalar.copy
     with ExitStack() as ctx:
         sb = ctx.enter_context(tc.tile_pool(name="sb", bufs=1))
         psum = ctx.enter_context(tc.psum_pool(name="psum", bufs=1))
@@ -35,239 +39,222 @@ def tile_mix_linattn_fm_pl_relu2_kernel(tc, qc, kc, qd, st, vc_words, vc_scales,
         def bank(number, name):
             return psum.tile([P, T], F32, name=name, tag="bank%d" % number)
 
-        vcw_raw = tile("vcw_raw", [P, 2 * M], U8)
-        vcs_raw = tile("vcs_raw", [P, M], U8)
-        vcw = tile("vcw", [P, 2 * M], U8)
-        vcs = tile("vcs", [P, M], U8)
-        kc_raw = tile("kc_raw", [P, PACK, T], F32)
-        qc_raw = tile("qc_raw", [P, PACK, T], F32)
-        dm_raw = tile("dm_raw", [P, PACK, T], F32)
-        qd_raw = tile("qd_raw", [P, PACK, T], F32)
-        st_raw = [tile("st_raw%d" % a, [P, PACK, GROUP], F32) for a in range(GROUPS)]
-        names = ["kc", "qc", "qd", "h"] + ["st%d" % a for a in range(GROUPS)] + ["o%d" % a for a in range(GROUPS)]
-        grouped = {n: tile(n + "_bf", [P, PACK * T], BF16) for n in names}
-        codes = {n: tile(n + "_codes", [P, T], U32) for n in names}
-        scales = {n: tile(n + "_scales", [P, T], U8) for n in names[:7]}
+        def four_rows(dram):
+            return dram.rearrange("(p j) w -> p j w", j=PACK)
+
+        vc_words_raw = tile("vc_words_raw", [P, 2 * M], U8)
+        vc_scales_raw = tile("vc_scales_raw", [P, M], U8)
+        vc_words_dealt = tile("vc_words_dealt", [P, 2 * M], U8)
+        vc_scales_dealt = tile("vc_scales_dealt", [P, M], U8)
+        states = ["st%d" % a for a in range(GROUPS)]
+        outs = ["out%d" % a for a in range(GROUPS)]
+        source = {name: tile(name + "_f32", [P, PACK, T], F32) for name in ["kc", "qc", "dm", "qd"] + states}
+        made = ["kc", "qc", "qd", "h"] + states
+        rounded = {name: tile(name + "_bf16", [P, PACK * T], BF16) for name in made + outs}
+        codes = {name: tile(name + "_codes", [P, T], U32) for name in made + outs}
+        scales = {name: tile(name + "_scales", [P, T], U8)[:] for name in made}
         out_scales = tile("out_scales", [P, GROUPS, T], U8)
         relu = [tile("relu%d" % a, [P, PACK, T], F32) for a in range(GROUPS)]
-        result = [tile("result%d" % a, [P, PACK, T], F32) for a in range(GROUPS)]
-        warm = tile("warm", [P, 8], F32)
-        hbank = {}
-        ybank = {}
+        for a in range(GROUPS):
+            source[outs[a]] = tile(outs[a] + "_f32", [P, PACK, T], F32)
+            scales[outs[a]] = out_scales[:, a, :]
+        h_bank = {}
+        y_bank = {}
 
-        def rows4(ap):
-            return ap.rearrange("(p j) w -> p j w", j=PACK)
+        nc.vector.memset(vc_scales_raw[:].bitcast(I32), 0)
+        nc.sync.dma_start(out=vc_words_raw[:].bitcast(I32), in_=vc_words[0].bitcast(I32))
+        for q in range(P // QUADRANT):
+            nc.sync.dma_start(
+                out=vc_scales_raw[QUADRANT * q : QUADRANT * q + 4, :].bitcast(I32),
+                in_=vc_scales[0, 4 * q : 4 * q + 4, :].bitcast(I32),
+            )
+        state_columns = [st[:, a * GROUP : (a + 1) * GROUP] for a in range(GROUPS)]
+        for name, dram in [("kc", kc), ("qc", qc), ("dm", dm), ("st0", state_columns[0]), ("qd", qd), ("st1", state_columns[1]), ("st2", state_columns[2])]:
+            nc.sync.dma_start(out=source[name][:], in_=four_rows(dram))
 
-        nc.vector.memset(vcs_raw[:].bitcast(I32), 0)
-        nc.vector.memset(warm[:], 0.0)
-        nc.sync.dma_start(out=vcw_raw[:].bitcast(I32), in_=vc_words[0].bitcast(I32))
-        nc.sync.dma_start(out=kc_raw[:], in_=rows4(kc))
-        for q in range(4):
-            nc.sync.dma_start(out=vcs_raw[32 * q : 32 * q + 4, :].bitcast(I32), in_=vc_scales[0, 4 * q : 4 * q + 4, :].bitcast(I32))
-        nc.scalar.activation(out=warm[:], in_=warm[:], func=ACT.Relu)
-        nc.sync.dma_start(out=qc_raw[:], in_=rows4(qc))
-        nc.sync.dma_start(out=dm_raw[:], in_=rows4(dm))
-        nc.sync.dma_start(out=st_raw[0][:], in_=rows4(st[:, 0:GROUP]))
-        nc.sync.dma_start(out=qd_raw[:], in_=rows4(qd))
-        for a in range(1, GROUPS):
-            nc.sync.dma_start(out=st_raw[a][:], in_=rows4(st[:, a * GROUP : (a + 1) * GROUP]))
+        def deal_vc_words(a):
+            span = slice(2 * GROUP * a, 2 * GROUP * (a + 1))
+            nc.vector.tensor_copy(
+                out=vc_words_dealt[:, span].rearrange("p (r m b) -> p r m b", r=PACK, b=2),
+                in_=vc_words_raw[:, span].rearrange("p (m r b) -> p r m b", r=PACK, b=2),
+            )
 
-        def copy(engine, out, in_):
-            if engine == "V":
-                nc.vector.tensor_copy(out=out, in_=in_)
-            else:
-                nc.scalar.copy(out=out, in_=in_)
+        def deal_vc_scales():
+            nc.vector.tensor_copy(
+                out=vc_scales_dealt[:].rearrange("p (a r m) -> p r a m", a=GROUPS, r=PACK),
+                in_=vc_scales_raw[:].rearrange("p (a m r) -> p r a m", a=GROUPS, r=PACK),
+            )
 
-        def deal_words(a):
-            src = vcw_raw[:, 2 * GROUP * a : 2 * GROUP * (a + 1)].rearrange("p (m r b) -> p r m b", r=PACK, b=2)
-            dst = vcw[:, 2 * GROUP * a : 2 * GROUP * (a + 1)].rearrange("p (r m b) -> p r m b", r=PACK, b=2)
-            nc.vector.tensor_copy(out=dst, in_=src)
+        def round_dealt(copy, name, m0, m1):
+            copy(
+                out=rounded[name][:].rearrange("p (r m j) -> p m j r", r=PACK, j=PACK)[:, m0:m1],
+                in_=source[name][:, :, PACK * m0 : PACK * m1].rearrange("p j (m r) -> p m j r", r=PACK),
+            )
 
-        def deal_scales():
-            src = vcs_raw[:].rearrange("p (a m r) -> p r a m", a=GROUPS, r=PACK)
-            dst = vcs[:].rearrange("p (a r m) -> p r a m", a=GROUPS, r=PACK)
-            nc.vector.tensor_copy(out=dst, in_=src)
+        def round_plain(copy, name, c0, c1):
+            copy(
+                out=rounded[name][:, PACK * c0 : PACK * c1].rearrange("p (c i j) -> p c j i", i=PACK, j=PACK),
+                in_=source[name][:, :, c0:c1].rearrange("p j (c i) -> p c j i", i=PACK),
+            )
 
-        def cast_dealt(engine, name, raw, raw_m0, m0, m1):
-            src = raw[:, :, PACK * (m0 - raw_m0) : PACK * (m1 - raw_m0)].rearrange("p j (m r) -> p m r j", r=PACK)
-            dst = grouped[name][:].rearrange("p (r m j) -> p m r j", r=PACK, j=PACK)[:, m0:m1]
-            copy(engine, dst, src)
+        def quantise(name, c0=0, c1=T):
+            nc.vector.quantize_mx(
+                out=codes[name][:, c0:c1].bitcast(FP8X4),
+                scales=scales[name][:, c0:c1],
+                in_=rounded[name][:, PACK * c0 : PACK * c1],
+            )
 
-        def cast_plain(engine, name, raw, raw_c0, c0, c1):
-            src = raw[:, :, c0 - raw_c0 : c1 - raw_c0].rearrange("p j (c i) -> p c j i", i=PACK)
-            dst = grouped[name][:, PACK * c0 : PACK * c1].rearrange("p (c i j) -> p c j i", i=PACK, j=PACK)
-            copy(engine, dst, src)
-
-        def quant(name, c0, c1, plane=None):
-            if plane is None:
-                plane = scales[name][:, c0:c1]
-            nc.vector.quantize_mx(out=codes[name][:, c0:c1].bitcast(FP8X4), scales=plane, in_=grouped[name][:, PACK * c0 : PACK * c1])
-
-        def h_matmuls(tb):
-            hbank[tb] = bank(tb, "hbank%d" % tb)
-            cols = slice(tb * P, (tb + 1) * P)
-            for i in range(PACK):
-                keys = slice(i * P, (i + 1) * P)
+        def h_sums(tb):
+            h_bank[tb] = bank(tb, "h_bank%d" % tb)
+            queries = slice(tb * P, (tb + 1) * P)
+            for r in range(PACK):
+                run = slice(r * P, (r + 1) * P)
                 nc.tensor.matmul_mx(
-                    out=hbank[tb][:, keys],
-                    lhsT=codes["kc"][:, keys].bitcast(FP8X4),
-                    lhsT_scale=scales["kc"][:, keys],
-                    rhs=codes["qc"][:, cols].bitcast(FP8X4),
-                    rhs_scale=scales["qc"][:, cols],
+                    out=h_bank[tb][:, run],
+                    lhsT=codes["kc"][:, run].bitcast(FP8X4),
+                    lhsT_scale=scales["kc"][:, run],
+                    rhs=codes["qc"][:, queries].bitcast(FP8X4),
+                    rhs_scale=scales["qc"][:, queries],
                     start=True,
                     stop=True,
                 )
 
         def h_decay(tb):
             nc.vector.tensor_tensor(
-                out=grouped["h"][:, GROUP * tb : GROUP * (tb + 1)].rearrange("p (t i) -> p t i", i=PACK),
-                in0=hbank[tb][:].rearrange("p (i t) -> p t i", i=PACK),
-                in1=dm_raw[:, :, tb * P : (tb + 1) * P].rearrange("p i t -> p t i"),
+                out=rounded["h"][:, GROUP * tb : GROUP * (tb + 1)].rearrange("p (t r) -> p t r", r=PACK),
+                in0=h_bank[tb][:].rearrange("p (r t) -> p t r", r=PACK),
+                in1=source["dm"][:, :, tb * P : (tb + 1) * P].rearrange("p r t -> p t r"),
                 op=ALU.mult,
             )
 
-        def y_values(a, r):
-            ybank[a, r] = bank((PACK * (a + 1) + r) % 8, "ybank%d_%d" % (a, r))
+        def y_open(a, r):
+            y_bank[a, r] = bank((PACK * (a + 1) + r) % BANKS, "y_bank%d_%d" % (a, r))
             col = a * GROUP + r * P
             nc.tensor.matmul_mx(
-                out=ybank[a, r][:],
-                lhsT=vcw[:, 2 * col : 2 * (col + P)].bitcast(FP4X4),
-                lhsT_scale=vcs[:, col : col + P],
+                out=y_bank[a, r][:],
+                lhsT=vc_words_dealt[:, 2 * col : 2 * (col + P)].bitcast(FP4X4),
+                lhsT_scale=vc_scales_dealt[:, col : col + P],
                 rhs=codes["h"][:].bitcast(FP8X4),
-                rhs_scale=scales["h"][:],
+                rhs_scale=scales["h"],
                 start=True,
                 stop=False,
             )
 
-        def y_state(a, r):
-            name = "st%d" % a
-            cols = slice(r * P, (r + 1) * P)
-            nc.tensor.matmul_mx(
-                out=ybank[a, r][:],
-                lhsT=codes[name][:, cols].bitcast(FP8X4),
-                lhsT_scale=scales[name][:, cols],
-                rhs=codes["qd"][:].bitcast(FP8X4),
-                rhs_scale=scales["qd"][:],
-                start=False,
-                stop=True,
-            )
+        def y_close(a):
+            for r in range(PACK):
+                run = slice(r * P, (r + 1) * P)
+                nc.tensor.matmul_mx(
+                    out=y_bank[a, r][:],
+                    lhsT=codes[states[a]][:, run].bitcast(FP8X4),
+                    lhsT_scale=scales[states[a]][:, run],
+                    rhs=codes["qd"][:].bitcast(FP8X4),
+                    rhs_scale=scales["qd"],
+                    start=False,
+                    stop=True,
+                )
 
-        def step_relu(engine, a, r, c0=0, c1=T):
-            if engine == "V":
-                nc.vector.tensor_scalar(out=relu[a][:, r, c0:c1], in0=ybank[a, r][:, c0:c1], scalar1=0.0, scalar2=None, op0=ALU.max)
-            else:
-                nc.scalar.activation(out=relu[a][:, r, c0:c1], in_=ybank[a, r][:, c0:c1], func=ACT.Relu)
+        def relu_on_scalar(a):
+            for r in range(PACK - 1):
+                nc.scalar.activation(out=relu[a][:, r, :], in_=y_bank[a, r][:], func=ACT.Relu)
 
-        def step_square(engine, a, r0, r1, c0=0, c1=T):
-            if engine == "V":
-                nc.vector.tensor_tensor(out=result[a][:, r0:r1, c0:c1], in0=relu[a][:, r0:r1, c0:c1], in1=relu[a][:, r0:r1, c0:c1], op=ALU.mult)
-            else:
-                nc.scalar.activation(out=result[a][:, r0:r1, c0:c1], in_=relu[a][:, r0:r1, c0:c1], func=ACT.Square)
+        def relu_on_vector(a):
+            r = PACK - 1
+            nc.vector.tensor_scalar(out=relu[a][:, r, :], in0=y_bank[a, r][:], scalar1=0.0, scalar2=None, op0=ALU.max)
 
-        def store_result(a, r0, r1, c0=0, c1=T):
-            nc.sync.dma_start(out=rows4(out_0[a * GROUP : (a + 1) * GROUP, :])[:, r0:r1, c0:c1], in_=result[a][:, r0:r1, c0:c1])
+        def store_pair(a, pair):
+            rows = slice(2 * pair, 2 * pair + 2)
+            nc.sync.dma_start(out=four_rows(out_0[a * GROUP : (a + 1) * GROUP, :])[:, rows, :], in_=source[outs[a]][:, rows, :])
 
-        def out_cast(a, c0, c1):
-            cast_plain("V", "o%d" % a, result[a], 0, c0, c1)
+        def square_on_scalar(a, pair):
+            rows = slice(2 * pair, 2 * pair + 2)
+            nc.scalar.activation(out=source[outs[a]][:, rows, :], in_=relu[a][:, rows, :], func=ACT.Square)
+            store_pair(a, pair)
 
-        def out_quant(a, c0, c1):
-            quant("o%d" % a, c0, c1, out_scales[:, a, c0:c1])
+        def square_on_vector(a, pair):
+            rows = slice(2 * pair, 2 * pair + 2)
+            nc.vector.tensor_tensor(out=source[outs[a]][:, rows, :], in0=relu[a][:, rows, :], in1=relu[a][:, rows, :], op=ALU.mult)
+            store_pair(a, pair)
 
-        def store_words(a, c0, c1):
-            nc.sync.dma_start(
-                out=out_1[a].rearrange("p t i -> p (t i)")[:, PACK * c0 : PACK * c1].bitcast(I32),
-                in_=codes["o%d" % a][:, c0:c1].bitcast(I32),
-            )
+        def store_codes(a):
+            nc.sync.dma_start(out=out_1[a].rearrange("p t i -> p (t i)").bitcast(I32), in_=codes[outs[a]][:].bitcast(I32))
 
-        def store_scales(q, queue):
+        deal_vc_words(0)
+        deal_vc_scales()
+        deal_vc_words(1)
+        round_dealt(scalar, "kc", P // 2, P)
+        round_dealt(vector, "kc", 0, P // 2)
+        deal_vc_words(2)
+        round_plain(scalar, "qc", QUARTER, HALF)
+        round_plain(scalar, "qc", HALF + QUARTER, T)
+        round_plain(vector, "qc", 0, QUARTER)
+        quantise("kc")
+        quantise("qc", 0, HALF)
+        h_sums(0)
+        h_sums(1)
+        round_plain(vector, "qc", HALF, HALF + QUARTER)
+        quantise("qc", HALF, T)
+        h_sums(2)
+        h_sums(3)
+        for tb in range(T // P):
+            h_decay(tb)
+        round_dealt(scalar, "st0", P // 2, P)
+        round_dealt(vector, "st0", 0, P // 2)
+        quantise("h")
+        for r in range(PACK):
+            y_open(0, r)
+        y_open(1, 0)
+        quantise("st0")
+        round_plain(scalar, "qd", HALF + QUARTER, T)
+        round_plain(vector, "qd", HALF, HALF + QUARTER)
+        round_plain(vector, "qd", 0, HALF)
+        quantise("qd", HALF, T)
+        quantise("qd", 0, HALF)
+        y_close(0)
+        for r in range(1, PACK):
+            y_open(1, r)
+
+        round_dealt(vector, "st1", 0, P)
+        relu_on_scalar(0)
+        relu_on_vector(0)
+        y_open(2, 0)
+        square_on_scalar(0, 0)
+        quantise("st1")
+        y_close(1)
+        for r in range(1, PACK):
+            y_open(2, r)
+        round_dealt(vector, "st2", 0, P)
+        square_on_scalar(0, 1)
+        round_plain(vector, "out0", 0, HALF)
+        quantise("st2")
+        y_close(2)
+
+        relu_on_scalar(1)
+        relu_on_vector(1)
+        square_on_scalar(1, 0)
+        round_plain(vector, "out0", HALF, T)
+        quantise("out0", 0, HALF)
+        quantise("out0", HALF, T)
+        store_codes(0)
+        square_on_vector(1, 1)
+
+        relu_on_scalar(2)
+        relu_on_vector(2)
+        square_on_scalar(2, 0)
+        round_plain(vector, "out1", 0, HALF)
+        round_plain(vector, "out1", HALF, T)
+        square_on_scalar(2, 1)
+        quantise("out1", 0, HALF)
+        round_plain(scalar, "out2", LAST_SPLIT, T)
+        round_plain(vector, "out2", 0, LAST_SPLIT)
+        quantise("out1", HALF, T)
+        store_codes(1)
+        quantise("out2", 0, HALF)
+        quantise("out2", HALF, T)
+        store_codes(2)
+
+        for q in range(P // QUADRANT):
+            queue = nc.scalar if q % 2 else nc.sync
             queue.dma_start(
                 out=out_2.rearrange("a q t -> q a t")[4 * q : 4 * q + 4].bitcast(I32),
-                in_=out_scales[32 * q : 32 * q + 4].bitcast(I32),
+                in_=out_scales[QUADRANT * q : QUADRANT * q + 4].bitcast(I32),
             )
-
-        for a in range(GROUPS):
-            deal_words(a)
-        cast_dealt("S", "kc", kc_raw, 0, 16, P)
-        cast_dealt("V", "kc", kc_raw, 0, 0, 16)
-        deal_scales()
-        cast_plain("S", "qc", qc_raw, 0, 128, HALF)
-        cast_plain("S", "qc", qc_raw, 0, HALF, T)
-        quant("kc", 0, T)
-        cast_plain("V", "qc", qc_raw, 0, 0, 128)
-        quant("qc", 0, HALF)
-        h_matmuls(0)
-        h_matmuls(1)
-        quant("qc", HALF, T)
-        h_matmuls(2)
-        h_matmuls(3)
-        for tb in range(4):
-            h_decay(tb)
-        cast_dealt("S", "st0", st_raw[0], 0, 48, P)
-        cast_dealt("V", "st0", st_raw[0], 0, 0, 48)
-        quant("h", 0, T)
-        for r in range(PACK):
-            y_values(0, r)
-        y_values(1, 0)
-        y_values(1, 1)
-        quant("st0", 0, T)
-        cast_plain("S", "qd", qd_raw, 0, 384, T)
-        cast_plain("V", "qd", qd_raw, 0, HALF, 384)
-        cast_plain("V", "qd", qd_raw, 0, 0, HALF)
-        quant("qd", HALF, T)
-        quant("qd", 0, HALF)
-        for r in range(PACK):
-            y_state(0, r)
-        y_values(1, 2)
-        y_values(1, 3)
-        cast_dealt("V", "st1", st_raw[1], 0, 0, P)
-        step_relu("S", 0, 0)
-        step_relu("S", 0, 1)
-        step_relu("S", 0, 2)
-        step_relu("V", 0, 3)
-        for r in range(3):
-            y_values(2, r)
-        step_square("S", 0, 0, 2)
-        store_result(0, 0, 2)
-        quant("st1", 0, T)
-        for r in range(PACK):
-            y_state(1, r)
-        y_values(2, 3)
-        cast_dealt("V", "st2", st_raw[2], 0, 0, P)
-        step_square("S", 0, 2, 4)
-        store_result(0, 2, 4)
-        cast_plain("V", "o0", result[0], 0, 0, HALF)
-        quant("st2", 0, T)
-        for r in range(PACK):
-            y_state(2, r)
-        step_relu("S", 1, 0)
-        step_relu("S", 1, 1)
-        step_relu("S", 1, 2)
-        step_relu("V", 1, 3)
-        step_square("S", 1, 0, 2)
-        store_result(1, 0, 2)
-        cast_plain("V", "o0", result[0], 0, HALF, T)
-        out_quant(0, 0, HALF)
-        out_quant(0, HALF, T)
-        store_words(0, 0, T)
-        step_square("V", 1, 2, 4)
-        store_result(1, 2, 4)
-        step_relu("S", 2, 0)
-        step_relu("S", 2, 1)
-        step_relu("S", 2, 2)
-        step_relu("V", 2, 3)
-        step_square("S", 2, 0, 2)
-        store_result(2, 0, 2)
-        cast_plain("V", "o1", result[1], 0, 0, HALF)
-        cast_plain("V", "o1", result[1], 0, HALF, T)
-        step_square("S", 2, 2, 4)
-        store_result(2, 2, 4)
-        out_quant(1, 0, HALF)
-        cast_plain("S", "o2", result[2], 0, HALF, T)
-        cast_plain("V", "o2", result[2], 0, 0, HALF)
-        out_quant(1, HALF, T)
-        store_words(1, 0, T)
-        out_quant(2, 0, HALF)
-        out_quant(2, HALF, T)
-        store_words(2, 0, T)
-        for q in range(4):
-            store_scales(q, nc.scalar if q % 2 else nc.sync)

@@ -8,6 +8,7 @@ FLOPS = 2 * K * T * T + 2 * T * M * T + 2 * K * M * T
 F32 = mybir.dt.float32
 BF16 = mybir.dt.bfloat16
 U32 = mybir.dt.uint32
+U16 = mybir.dt.uint16
 I32 = mybir.dt.int32
 U8 = mybir.dt.uint8
 FP8X4 = mybir.dt.float8_e4m3fn_x4
@@ -21,8 +22,8 @@ GROUP = P * PACK
 GROUPS = M // GROUP
 BANKS = 8
 QUADRANT = 32
-QUARTER, HALF = T // 4, T // 2
-LAST_SPLIT = 320
+HALF = T // 2
+RUN = P // 2
 
 
 def tile_mix_linattn_fm_pl_relu2_kernel(tc, qc, kc, qd, st, vc_words, vc_scales, dm, out_0, out_1, out_2):
@@ -42,59 +43,67 @@ def tile_mix_linattn_fm_pl_relu2_kernel(tc, qc, kc, qd, st, vc_words, vc_scales,
         def four_rows(dram):
             return dram.rearrange("(p j) w -> p j w", j=PACK)
 
-        vc_words_raw = tile("vc_words_raw", [P, 2 * M], U8)
+        vc_words_raw = [tile("vc_words_raw%d" % a, [P, GROUP], U16) for a in range(GROUPS)]
+        vc_words_dealt = [tile("vc_words_dealt%d" % a, [P, GROUP], U16) for a in range(GROUPS)]
         vc_scales_raw = tile("vc_scales_raw", [P, M], U8)
-        vc_words_dealt = tile("vc_words_dealt", [P, 2 * M], U8)
         vc_scales_dealt = tile("vc_scales_dealt", [P, M], U8)
         states = ["st%d" % a for a in range(GROUPS)]
         outs = ["out%d" % a for a in range(GROUPS)]
-        source = {name: tile(name + "_f32", [P, PACK, T], F32) for name in ["kc", "qc", "dm", "qd"] + states}
+        dram = {"kc": kc, "qc": qc, "qd": qd, "dm": dm}
+        for a in range(GROUPS):
+            dram[states[a]] = st[:, a * GROUP : (a + 1) * GROUP]
         made = ["kc", "qc", "qd", "h"] + states
         rounded = {name: tile(name + "_bf16", [P, PACK * T], BF16) for name in made + outs}
         codes = {name: tile(name + "_codes", [P, T], U32) for name in made + outs}
         scales = {name: tile(name + "_scales", [P, T], U8)[:] for name in made}
         out_scales = tile("out_scales", [P, GROUPS, T], U8)
         relu = [tile("relu%d" % a, [P, PACK, T], F32) for a in range(GROUPS)]
+        pieces = {name: [] for name in dram}
         for a in range(GROUPS):
-            source[outs[a]] = tile(outs[a] + "_f32", [P, PACK, T], F32)
             scales[outs[a]] = out_scales[:, a, :]
+            pieces[outs[a]] = [(0, tile(outs[a] + "_f32", [P, PACK, T], F32))]
         h_bank = {}
         y_bank = {}
 
-        nc.vector.memset(vc_scales_raw[:].bitcast(I32), 0)
-        nc.sync.dma_start(out=vc_words_raw[:].bitcast(I32), in_=vc_words[0].bitcast(I32))
-        for q in range(P // QUADRANT):
-            nc.sync.dma_start(
-                out=vc_scales_raw[QUADRANT * q : QUADRANT * q + 4, :].bitcast(I32),
-                in_=vc_scales[0, 4 * q : 4 * q + 4, :].bitcast(I32),
-            )
-        state_columns = [st[:, a * GROUP : (a + 1) * GROUP] for a in range(GROUPS)]
-        for name, dram in [("kc", kc), ("qc", qc), ("dm", dm), ("st0", state_columns[0]), ("qd", qd), ("st1", state_columns[1]), ("st2", state_columns[2])]:
-            nc.sync.dma_start(out=source[name][:], in_=four_rows(dram))
+        def source(name, c0, c1):
+            first, piece = [entry for entry in pieces[name] if entry[0] <= c0][-1]
+            return piece[:, :, c0 - first : c1 - first]
+
+        def load(name, c0, c1, partitions=P):
+            piece = tile("%s_%d_f32" % (name, c0), [P, PACK, c1 - c0], F32)
+            pieces[name].append((c0, piece))
+            nc.sync.dma_start(out=piece[:partitions], in_=four_rows(dram[name][:, c0:c1])[:partitions])
+
+        def load_vc_words(a):
+            nc.sync.dma_start(out=vc_words_raw[a][:].bitcast(I32), in_=vc_words[0][:, 2 * GROUP * a : 2 * GROUP * (a + 1)].bitcast(I32))
+
+        def load_vc_scales():
+            for r in range(4):
+                nc.sync.dma_start(out=vc_scales_raw[r:P:QUADRANT, :].bitcast(I32), in_=vc_scales[0, r:16:4, :].bitcast(I32))
 
         def deal_vc_words(a):
-            span = slice(2 * GROUP * a, 2 * GROUP * (a + 1))
             nc.vector.tensor_copy(
-                out=vc_words_dealt[:, span].rearrange("p (r m b) -> p r m b", r=PACK, b=2),
-                in_=vc_words_raw[:, span].rearrange("p (m r b) -> p r m b", r=PACK, b=2),
+                out=vc_words_dealt[a][:].rearrange("p (r m) -> p m r", r=PACK),
+                in_=vc_words_raw[a][:].rearrange("p (m r) -> p m r", r=PACK),
             )
 
-        def deal_vc_scales():
+        def deal_vc_scales(a):
+            span = slice(a * GROUP, (a + 1) * GROUP)
             nc.vector.tensor_copy(
-                out=vc_scales_dealt[:].rearrange("p (a r m) -> p r a m", a=GROUPS, r=PACK),
-                in_=vc_scales_raw[:].rearrange("p (a m r) -> p r a m", a=GROUPS, r=PACK),
+                out=vc_scales_dealt[:, span].rearrange("p (r m) -> p r m", r=PACK),
+                in_=vc_scales_raw[:, span].rearrange("p (m r) -> p r m", r=PACK),
             )
 
-        def round_dealt(copy, name, m0, m1):
+        def round_dealt(copy, name, c0, c1):
             copy(
-                out=rounded[name][:].rearrange("p (r m j) -> p m j r", r=PACK, j=PACK)[:, m0:m1],
-                in_=source[name][:, :, PACK * m0 : PACK * m1].rearrange("p j (m r) -> p m j r", r=PACK),
+                out=rounded[name][:].rearrange("p (r m j) -> p m j r", r=PACK, j=PACK)[:, c0 // PACK : c1 // PACK],
+                in_=source(name, c0, c1).rearrange("p j (m r) -> p m j r", r=PACK),
             )
 
         def round_plain(copy, name, c0, c1):
             copy(
                 out=rounded[name][:, PACK * c0 : PACK * c1].rearrange("p (c i j) -> p c j i", i=PACK, j=PACK),
-                in_=source[name][:, :, c0:c1].rearrange("p j (c i) -> p c j i", i=PACK),
+                in_=source(name, c0, c1).rearrange("p j (c i) -> p c j i", i=PACK),
             )
 
         def quantise(name, c0=0, c1=T):
@@ -104,157 +113,206 @@ def tile_mix_linattn_fm_pl_relu2_kernel(tc, qc, kc, qd, st, vc_words, vc_scales,
                 in_=rounded[name][:, PACK * c0 : PACK * c1],
             )
 
-        def h_sums(tb):
-            h_bank[tb] = bank(tb, "h_bank%d" % tb)
+        def quantise_keys(hf):
+            for r in range(PACK):
+                quantise("kc", r * P + hf * RUN, r * P + (hf + 1) * RUN)
+
+        def mx_pass(out, stationary, stationary_scale, name, tb, start, stop):
             queries = slice(tb * P, (tb + 1) * P)
+            nc.tensor.matmul_mx(
+                out=out,
+                lhsT=stationary,
+                lhsT_scale=stationary_scale,
+                rhs=codes[name][:, queries].bitcast(FP8X4),
+                rhs_scale=scales[name][:, queries],
+                start=start,
+                stop=stop,
+            )
+
+        def h_sums(tb, number):
+            h_bank[tb] = bank(number, "h_bank%d" % tb)
             for r in range(PACK):
                 run = slice(r * P, (r + 1) * P)
-                nc.tensor.matmul_mx(
-                    out=h_bank[tb][:, run],
-                    lhsT=codes["kc"][:, run].bitcast(FP8X4),
-                    lhsT_scale=scales["kc"][:, run],
-                    rhs=codes["qc"][:, queries].bitcast(FP8X4),
-                    rhs_scale=scales["qc"][:, queries],
-                    start=True,
-                    stop=True,
-                )
+                mx_pass(h_bank[tb][:, run], codes["kc"][:, run].bitcast(FP8X4), scales["kc"][:, run], "qc", tb, True, True)
 
-        def h_decay(tb):
+        def h_decay(tb, partitions=P):
             nc.vector.tensor_tensor(
-                out=rounded["h"][:, GROUP * tb : GROUP * (tb + 1)].rearrange("p (t r) -> p t r", r=PACK),
-                in0=h_bank[tb][:].rearrange("p (r t) -> p t r", r=PACK),
-                in1=source["dm"][:, :, tb * P : (tb + 1) * P].rearrange("p r t -> p t r"),
+                out=rounded["h"][:partitions, GROUP * tb : GROUP * (tb + 1)].rearrange("p (c i r) -> p c r i", i=PACK, r=PACK),
+                in0=h_bank[tb][:partitions, :].rearrange("p (r c i) -> p c r i", r=PACK, i=PACK),
+                in1=source("dm", tb * P, (tb + 1) * P)[:partitions].rearrange("p r (c i) -> p c r i", i=PACK),
                 op=ALU.mult,
             )
 
-        def y_open(a, r):
-            y_bank[a, r] = bank((PACK * (a + 1) + r) % BANKS, "y_bank%d_%d" % (a, r))
-            col = a * GROUP + r * P
-            nc.tensor.matmul_mx(
-                out=y_bank[a, r][:],
-                lhsT=vc_words_dealt[:, 2 * col : 2 * (col + P)].bitcast(FP4X4),
-                lhsT_scale=vc_scales_dealt[:, col : col + P],
-                rhs=codes["h"][:].bitcast(FP8X4),
-                rhs_scale=scales["h"],
-                start=True,
-                stop=False,
-            )
+        def y_open(a, tb, number):
+            y_bank[a, tb] = bank(number, "y_bank%d%d" % (a, tb))
 
-        def y_close(a):
+        def y_values(a, tb, first):
             for r in range(PACK):
                 run = slice(r * P, (r + 1) * P)
-                nc.tensor.matmul_mx(
-                    out=y_bank[a, r][:],
-                    lhsT=codes[states[a]][:, run].bitcast(FP8X4),
-                    lhsT_scale=scales[states[a]][:, run],
-                    rhs=codes["qd"][:].bitcast(FP8X4),
-                    rhs_scale=scales["qd"],
-                    start=False,
-                    stop=True,
-                )
+                col = a * GROUP + r * P
+                mx_pass(y_bank[a, tb][:, run], vc_words_dealt[a][:, run].bitcast(U8).bitcast(FP4X4), vc_scales_dealt[:, col : col + P], "h", tb, first and r == 0, not first and r == PACK - 1)
 
-        def relu_on_scalar(a):
-            for r in range(PACK - 1):
-                nc.scalar.activation(out=relu[a][:, r, :], in_=y_bank[a, r][:], func=ACT.Relu)
+        def y_state(a, tb, first):
+            for r in range(PACK):
+                run = slice(r * P, (r + 1) * P)
+                mx_pass(y_bank[a, tb][:, run], codes[states[a]][:, run].bitcast(FP8X4), scales[states[a]][:, run], "qd", tb, first and r == 0, not first and r == PACK - 1)
 
-        def relu_on_vector(a):
-            r = PACK - 1
-            nc.vector.tensor_scalar(out=relu[a][:, r, :], in0=y_bank[a, r][:], scalar1=0.0, scalar2=None, op0=ALU.max)
+        def relu_on_scalar(a, tb):
+            nc.scalar.activation(out=relu[a][:, :, tb * P : (tb + 1) * P], in_=y_bank[a, tb][:].rearrange("p (r t) -> p r t", r=PACK), func=ACT.Relu)
 
-        def store_pair(a, pair):
-            rows = slice(2 * pair, 2 * pair + 2)
-            nc.sync.dma_start(out=four_rows(out_0[a * GROUP : (a + 1) * GROUP, :])[:, rows, :], in_=source[outs[a]][:, rows, :])
+        def relu_on_vector(a, tb):
+            nc.vector.tensor_scalar(out=relu[a][:, :, tb * P : (tb + 1) * P], in0=y_bank[a, tb][:].rearrange("p (r t) -> p r t", r=PACK), scalar1=0.0, scalar2=None, op0=ALU.max)
 
-        def square_on_scalar(a, pair):
-            rows = slice(2 * pair, 2 * pair + 2)
-            nc.scalar.activation(out=source[outs[a]][:, rows, :], in_=relu[a][:, rows, :], func=ACT.Square)
-            store_pair(a, pair)
+        def square_on_scalar(a, c0, c1):
+            nc.scalar.activation(out=source(outs[a], c0, c1), in_=relu[a][:, :, c0:c1], func=ACT.Square)
 
-        def square_on_vector(a, pair):
-            rows = slice(2 * pair, 2 * pair + 2)
-            nc.vector.tensor_tensor(out=source[outs[a]][:, rows, :], in0=relu[a][:, rows, :], in1=relu[a][:, rows, :], op=ALU.mult)
-            store_pair(a, pair)
+        def square_on_vector(a, c0, c1):
+            nc.vector.tensor_tensor(out=source(outs[a], c0, c1), in0=relu[a][:, :, c0:c1], in1=relu[a][:, :, c0:c1], op=ALU.mult)
 
-        def store_codes(a):
-            nc.sync.dma_start(out=out_1[a].rearrange("p t i -> p (t i)").bitcast(I32), in_=codes[outs[a]][:].bitcast(I32))
+        def store_out(a, c0, c1):
+            nc.sync.dma_start(out=four_rows(out_0[a * GROUP : (a + 1) * GROUP, c0:c1]), in_=source(outs[a], c0, c1))
 
+        def store_codes(a, c0=0, c1=T):
+            nc.sync.dma_start(out=out_1[a].rearrange("p t i -> p (t i)").bitcast(I32)[:, c0:c1], in_=codes[outs[a]][:, c0:c1].bitcast(I32))
+
+        def store_scales(queue, r):
+            queue.dma_start(
+                out=out_2.rearrange("a q t -> q a t")[r:16:4].bitcast(I32),
+                in_=out_scales[r:P:QUADRANT].bitcast(I32),
+            )
+
+        nc.vector.memset(vc_scales_raw[:].bitcast(I32), 0)
+        nc.vector.memset(codes["kc"][:], 0)
+        nc.vector.memset(scales["kc"].bitcast(I32), 0)
+        nc.vector.memset(rounded["h"][RUN:, : PACK * HALF].bitcast(I32), 0)
+
+        Q2, Q3 = 2 * P, 3 * P
+        load("kc", 0, HALF)
+        load_vc_scales()
+        load("qc", 0, HALF)
+        load_vc_words(0)
+        load("dm", 0, HALF, RUN)
+        load("st0", 0, HALF)
+        load("st0", HALF, T)
+        load("qd", 0, HALF)
+        load_vc_words(1)
+        load("st1", 0, HALF)
+        load("st1", HALF, T)
+        load("kc", HALF, T)
+        load("qc", HALF, T)
+        load("qd", HALF, T)
+        load("dm", HALF, T)
+        load_vc_words(2)
+        load("st2", 0, HALF)
+        load("st2", HALF, T)
+
+        round_dealt(scalar, "kc", P, HALF)
+        round_dealt(vector, "kc", 0, P)
+        deal_vc_scales(0)
+        quantise_keys(0)
+        round_plain(scalar, "qc", P, HALF)
+        round_plain(vector, "qc", 0, P)
         deal_vc_words(0)
-        deal_vc_scales()
-        deal_vc_words(1)
-        round_dealt(scalar, "kc", P // 2, P)
-        round_dealt(vector, "kc", 0, P // 2)
-        deal_vc_words(2)
-        round_plain(scalar, "qc", QUARTER, HALF)
-        round_plain(scalar, "qc", HALF + QUARTER, T)
-        round_plain(vector, "qc", 0, QUARTER)
-        quantise("kc")
-        quantise("qc", 0, HALF)
-        h_sums(0)
-        h_sums(1)
-        round_plain(vector, "qc", HALF, HALF + QUARTER)
-        quantise("qc", HALF, T)
-        h_sums(2)
-        h_sums(3)
-        for tb in range(T // P):
-            h_decay(tb)
-        round_dealt(scalar, "st0", P // 2, P)
-        round_dealt(vector, "st0", 0, P // 2)
-        quantise("h")
-        for r in range(PACK):
-            y_open(0, r)
-        y_open(1, 0)
+        quantise("qc", 0, P)
+        quantise("qc", P, HALF)
+        h_sums(0, 0)
+        h_sums(1, 1)
+        deal_vc_scales(1)
+        deal_vc_scales(2)
+        h_decay(0, RUN)
+        h_decay(1, RUN)
+        quantise("h", 0, P)
+        quantise("h", P, HALF)
+        for tb in range(2):
+            y_open(0, tb, 2 + tb)
+            y_values(0, tb, True)
+        round_dealt(scalar, "st0", 0, HALF)
+        round_dealt(scalar, "st0", 432, T)
+        round_dealt(vector, "st0", HALF, 432)
+        round_plain(scalar, "qd", P, HALF)
         quantise("st0")
-        round_plain(scalar, "qd", HALF + QUARTER, T)
-        round_plain(vector, "qd", HALF, HALF + QUARTER)
-        round_plain(vector, "qd", 0, HALF)
-        quantise("qd", HALF, T)
-        quantise("qd", 0, HALF)
-        y_close(0)
-        for r in range(1, PACK):
-            y_open(1, r)
+        round_plain(vector, "qd", 0, P)
+        deal_vc_words(1)
+        quantise("qd", 0, P)
+        quantise("qd", P, HALF)
+        for tb in range(2):
+            y_state(0, tb, False)
+        for tb in range(2):
+            y_open(1, tb, 4 + tb)
+            y_values(1, tb, True)
 
-        round_dealt(vector, "st1", 0, P)
-        relu_on_scalar(0)
-        relu_on_vector(0)
-        y_open(2, 0)
-        square_on_scalar(0, 0)
+        round_dealt(scalar, "st1", 0, P)
+        round_dealt(vector, "st1", P, HALF)
+        round_dealt(vector, "st1", HALF, T)
+        relu_on_scalar(0, 0)
+        relu_on_scalar(0, 1)
+        square_on_scalar(0, 0, HALF)
         quantise("st1")
-        y_close(1)
-        for r in range(1, PACK):
-            y_open(2, r)
-        round_dealt(vector, "st2", 0, P)
-        square_on_scalar(0, 1)
-        round_plain(vector, "out0", 0, HALF)
-        quantise("st2")
-        y_close(2)
-
-        relu_on_scalar(1)
-        relu_on_vector(1)
-        square_on_scalar(1, 0)
-        round_plain(vector, "out0", HALF, T)
+        for tb in range(2):
+            y_state(1, tb, False)
+        round_dealt(vector, "kc", HALF, T)
+        relu_on_scalar(1, 0)
+        relu_on_scalar(1, 1)
+        round_plain(vector, "qc", HALF, T)
+        quantise_keys(1)
+        quantise("qc", Q2, Q3)
+        quantise("qc", Q3, T)
+        h_sums(2, 0)
+        h_sums(3, 1)
+        round_plain(scalar, "qd", Q3, T)
+        round_plain(vector, "qd", Q2, Q3)
+        square_on_scalar(1, 0, HALF)
+        round_plain(vector, "out0", 0, P)
+        quantise("qd", HALF, T)
+        late = [(0, 2), (0, 3), (1, 2), (1, 3)]
+        for n, (a, tb) in enumerate(late):
+            y_open(a, tb, 2 + n)
+            y_state(a, tb, True)
+        h_decay(2)
+        h_decay(3)
+        quantise("h", Q2, Q3)
+        quantise("h", Q3, T)
+        for a, tb in late:
+            y_values(a, tb, False)
+        deal_vc_words(2)
+        for tb in range(4):
+            y_open(2, tb, (6 + tb) % BANKS)
+            y_values(2, tb, True)
+        round_plain(scalar, "out0", P, HALF)
+        round_dealt(scalar, "st2", 0, HALF)
+        round_dealt(vector, "st2", HALF, T)
         quantise("out0", 0, HALF)
+        quantise("st2")
+        for tb in range(4):
+            y_state(2, tb, False)
+        store_out(0, 0, HALF)
+        store_out(1, 0, HALF)
+        relu_on_scalar(0, 2)
+        relu_on_scalar(0, 3)
+        relu_on_scalar(1, 2)
+        square_on_scalar(0, HALF, T)
+        store_out(0, HALF, T)
+        relu_on_vector(1, 3)
+        square_on_scalar(1, HALF, T)
+        store_out(1, HALF, T)
+        relu_on_vector(2, 0)
+        relu_on_vector(2, 1)
+        round_plain(vector, "out0", HALF, T)
+        relu_on_scalar(2, 2)
+        square_on_scalar(2, 0, HALF)
+        store_out(2, 0, HALF)
+        relu_on_vector(2, 3)
         quantise("out0", HALF, T)
         store_codes(0)
-        square_on_vector(1, 1)
-
-        relu_on_scalar(2)
-        relu_on_vector(2)
-        square_on_scalar(2, 0)
-        round_plain(vector, "out1", 0, HALF)
-        round_plain(vector, "out1", HALF, T)
-        square_on_scalar(2, 1)
-        quantise("out1", 0, HALF)
-        round_plain(scalar, "out2", LAST_SPLIT, T)
-        round_plain(vector, "out2", 0, LAST_SPLIT)
-        quantise("out1", HALF, T)
+        square_on_scalar(2, HALF, T)
+        store_out(2, HALF, T)
+        round_plain(vector, "out1", 0, T)
+        round_plain(vector, "out2", 0, HALF)
+        quantise("out1")
         store_codes(1)
+        round_plain(scalar, "out2", HALF, T)
         quantise("out2", 0, HALF)
         quantise("out2", HALF, T)
         store_codes(2)
-
-        for q in range(P // QUADRANT):
-            queue = nc.scalar if q % 2 else nc.sync
-            queue.dma_start(
-                out=out_2.rearrange("a q t -> q a t")[4 * q : 4 * q + 4].bitcast(I32),
-                in_=out_scales[QUADRANT * q : QUADRANT * q + 4].bitcast(I32),
-            )
+        for r in range(4):
+            store_scales(nc.scalar if r % 2 else nc.sync, r)

@@ -157,6 +157,47 @@ def tile_mix_linattn_fm_pl_relu2_kernel(tc, qc, kc, qd, st, vc_words, vc_scales,
                 run = slice(r * P, (r + 1) * P)
                 mx_pass(y_bank[a, tb][:, run], codes[states[a]][:, run].bitcast(FP8X4), scales[states[a]][:, run], "qd", tb, first and r == 0, not first and r == PACK - 1)
 
+        def rows_open(a, r, number):
+            y_bank[a, r] = bank(number, "y_bank%d%d" % (a, r))
+            run = slice(r * P, (r + 1) * P)
+            col = a * GROUP + r * P
+            nc.tensor.matmul_mx(
+                out=y_bank[a, r][:],
+                lhsT=vc_words_dealt[a][:, run].bitcast(U8).bitcast(FP4X4),
+                lhsT_scale=vc_scales_dealt[:, col : col + P],
+                rhs=codes["h"][:].bitcast(FP8X4),
+                rhs_scale=scales["h"],
+                start=True,
+                stop=False,
+            )
+
+        def rows_close(a, r):
+            run = slice(r * P, (r + 1) * P)
+            nc.tensor.matmul_mx(
+                out=y_bank[a, r][:],
+                lhsT=codes[states[a]][:, run].bitcast(FP8X4),
+                lhsT_scale=scales[states[a]][:, run],
+                rhs=codes["qd"][:].bitcast(FP8X4),
+                rhs_scale=scales["qd"],
+                start=False,
+                stop=True,
+            )
+
+        def relu_row_on_scalar(a, r):
+            nc.scalar.activation(out=relu[a][:, r, :], in_=y_bank[a, r][:], func=ACT.Relu)
+
+        def relu_row_on_vector(a, r):
+            nc.vector.tensor_scalar(out=relu[a][:, r, :], in0=y_bank[a, r][:], scalar1=0.0, scalar2=None, op0=ALU.max)
+
+        def square_rows_on_scalar(a, r0, r1):
+            nc.scalar.activation(out=source(outs[a], 0, T)[:, r0:r1, :], in_=relu[a][:, r0:r1, :], func=ACT.Square)
+
+        def square_rows_on_vector(a, r0, r1):
+            nc.vector.tensor_tensor(out=source(outs[a], 0, T)[:, r0:r1, :], in0=relu[a][:, r0:r1, :], in1=relu[a][:, r0:r1, :], op=ALU.mult)
+
+        def store_rows(a, r0, r1):
+            nc.sync.dma_start(out=four_rows(out_0[a * GROUP : (a + 1) * GROUP, :])[:, r0:r1, :], in_=source(outs[a], 0, T)[:, r0:r1, :])
+
         def relu_on_scalar(a, tb):
             nc.scalar.activation(out=relu[a][:, :, tb * P : (tb + 1) * P], in_=y_bank[a, tb][:].rearrange("p (r t) -> p r t", r=PACK), func=ACT.Relu)
 
@@ -175,144 +216,118 @@ def tile_mix_linattn_fm_pl_relu2_kernel(tc, qc, kc, qd, st, vc_words, vc_scales,
         def store_codes(a, c0=0, c1=T):
             nc.sync.dma_start(out=out_1[a].rearrange("p t i -> p (t i)").bitcast(I32)[:, c0:c1], in_=codes[outs[a]][:, c0:c1].bitcast(I32))
 
-        def store_scales(queue, r):
+        def store_scales(queue, r, a0, a1):
             queue.dma_start(
-                out=out_2.rearrange("a q t -> q a t")[r:16:4].bitcast(I32),
-                in_=out_scales[r:P:QUADRANT].bitcast(I32),
+                out=out_2.rearrange("a q t -> q a t")[r:16:4, a0:a1].bitcast(I32),
+                in_=out_scales[r:P:QUADRANT, a0:a1].bitcast(I32),
             )
 
         nc.vector.memset(vc_scales_raw[:].bitcast(I32), 0)
-        nc.vector.memset(codes["kc"][:], 0)
-        nc.vector.memset(scales["kc"].bitcast(I32), 0)
-        nc.vector.memset(rounded["h"][RUN:, : PACK * HALF].bitcast(I32), 0)
-
         Q2, Q3 = 2 * P, 3 * P
-        load("kc", 0, HALF)
-        load_vc_scales()
-        load("qc", 0, HALF)
         load_vc_words(0)
-        load("dm", 0, HALF, RUN)
-        load("st0", 0, HALF)
-        load("st0", HALF, T)
+        load("kc", 0, T)
+        load_vc_scales()
+        load("qc", 0, T)
+        load("dm", 0, T)
+        load("st0", 0, T)
         load("qd", 0, HALF)
-        load_vc_words(1)
-        load("st1", 0, HALF)
-        load("st1", HALF, T)
-        load("kc", HALF, T)
-        load("qc", HALF, T)
         load("qd", HALF, T)
-        load("dm", HALF, T)
-        load_vc_words(2)
-        load("st2", 0, HALF)
-        load("st2", HALF, T)
+        for a in range(1, GROUPS):
+            load_vc_words(a)
+            load(states[a], 0, T)
 
-        round_dealt(scalar, "kc", P, HALF)
-        round_dealt(vector, "kc", 0, P)
-        deal_vc_scales(0)
-        quantise_keys(0)
-        round_plain(scalar, "qc", P, HALF)
-        round_plain(vector, "qc", 0, P)
         deal_vc_words(0)
-        quantise("qc", 0, P)
-        quantise("qc", P, HALF)
-        h_sums(0, 0)
-        h_sums(1, 1)
+        round_dealt(scalar, "kc", HALF, T)
+        round_dealt(vector, "kc", 0, HALF)
+        deal_vc_scales(0)
         deal_vc_scales(1)
+        quantise("kc")
         deal_vc_scales(2)
-        h_decay(0, RUN)
-        h_decay(1, RUN)
-        quantise("h", 0, P)
-        quantise("h", P, HALF)
-        for tb in range(2):
-            y_open(0, tb, 2 + tb)
-            y_values(0, tb, True)
-        round_dealt(scalar, "st0", 0, HALF)
-        round_dealt(scalar, "st0", 432, T)
-        round_dealt(vector, "st0", HALF, 432)
-        round_plain(scalar, "qd", P, HALF)
-        quantise("st0")
-        round_plain(vector, "qd", 0, P)
-        deal_vc_words(1)
-        quantise("qd", 0, P)
-        quantise("qd", P, HALF)
-        for tb in range(2):
-            y_state(0, tb, False)
-        for tb in range(2):
-            y_open(1, tb, 4 + tb)
-            y_values(1, tb, True)
+        round_plain(scalar, "qc", P, HALF)
+        round_plain(scalar, "qc", Q3, T)
+        round_plain(vector, "qc", 0, P)
+        round_plain(vector, "qc", Q2, Q3)
+        for tb in range(4):
+            quantise("qc", tb * P, (tb + 1) * P)
+            h_sums(tb, tb)
 
-        round_dealt(scalar, "st1", 0, P)
-        round_dealt(vector, "st1", P, HALF)
-        round_dealt(vector, "st1", HALF, T)
+        def h_done(tb):
+            quantise("h", tb * P, (tb + 1) * P)
+            y_open(0, tb, 4 + tb)
+            y_values(0, tb, True)
+
+        h_decay(0)
+        h_decay(1)
+        h_done(0)
+        h_decay(2)
+        h_done(1)
+        round_dealt(scalar, "st0", HALF, T)
+        round_dealt(vector, "st0", 0, HALF)
+        h_done(2)
+        h_decay(3)
+        quantise("st0")
+        round_plain(scalar, "qd", 0, P)
+        round_plain(scalar, "qd", P, HALF)
+        round_plain(scalar, "qd", Q2, Q3)
+        quantise("qd", 0, P)
+        y_state(0, 0, False)
+        h_done(3)
+        quantise("qd", P, HALF)
+        y_state(0, 1, False)
+        round_plain(vector, "qd", Q3, T)
+        quantise("qd", Q2, Q3)
+        y_state(0, 2, False)
+        quantise("qd", Q3, T)
+        y_state(0, 3, False)
+        deal_vc_words(1)
+        for r in range(PACK):
+            rows_open(1, r, r)
         relu_on_scalar(0, 0)
         relu_on_scalar(0, 1)
-        square_on_scalar(0, 0, HALF)
-        quantise("st1")
-        for tb in range(2):
-            y_state(1, tb, False)
-        round_dealt(vector, "kc", HALF, T)
-        relu_on_scalar(1, 0)
-        relu_on_scalar(1, 1)
-        round_plain(vector, "qc", HALF, T)
-        quantise_keys(1)
-        quantise("qc", Q2, Q3)
-        quantise("qc", Q3, T)
-        h_sums(2, 0)
-        h_sums(3, 1)
-        round_plain(scalar, "qd", Q3, T)
-        round_plain(vector, "qd", Q2, Q3)
-        square_on_scalar(1, 0, HALF)
-        round_plain(vector, "out0", 0, P)
-        quantise("qd", HALF, T)
-        late = [(0, 2), (0, 3), (1, 2), (1, 3)]
-        for n, (a, tb) in enumerate(late):
-            y_open(a, tb, 2 + n)
-            y_state(a, tb, True)
-        h_decay(2)
-        h_decay(3)
-        quantise("h", Q2, Q3)
-        quantise("h", Q3, T)
-        for a, tb in late:
-            y_values(a, tb, False)
-        deal_vc_words(2)
-        for tb in range(4):
-            y_open(2, tb, (6 + tb) % BANKS)
-            y_values(2, tb, True)
-        round_plain(scalar, "out0", P, HALF)
-        round_dealt(scalar, "st2", 0, HALF)
-        round_dealt(vector, "st2", HALF, T)
-        quantise("out0", 0, HALF)
-        quantise("st2")
-        for tb in range(4):
-            y_state(2, tb, False)
+        square_on_vector(0, 0, P)
+        square_on_vector(0, P, HALF)
         store_out(0, 0, HALF)
-        store_out(1, 0, HALF)
         relu_on_scalar(0, 2)
         relu_on_scalar(0, 3)
-        relu_on_scalar(1, 2)
         square_on_scalar(0, HALF, T)
         store_out(0, HALF, T)
-        relu_on_vector(1, 3)
-        square_on_scalar(1, HALF, T)
-        store_out(1, HALF, T)
-        relu_on_vector(2, 0)
-        relu_on_vector(2, 1)
+        round_dealt(vector, "st1", 0, T)
+        deal_vc_words(2)
+        quantise("st1")
+        for r in range(PACK):
+            rows_close(1, r)
+        for r in range(PACK):
+            rows_open(2, r, 4 + r)
+        round_plain(scalar, "out0", 0, HALF)
         round_plain(vector, "out0", HALF, T)
-        relu_on_scalar(2, 2)
-        square_on_scalar(2, 0, HALF)
-        store_out(2, 0, HALF)
-        relu_on_vector(2, 3)
-        quantise("out0", HALF, T)
+        round_dealt(vector, "st2", 0, T)
+        quantise("out0")
         store_codes(0)
-        square_on_scalar(2, HALF, T)
-        store_out(2, HALF, T)
+        quantise("st2")
+        for r in range(PACK):
+            rows_close(2, r)
+        for r in range(PACK):
+            relu_row_on_scalar(1, r)
+        square_rows_on_vector(1, 0, 2)
+        store_rows(1, 0, 2)
+        square_rows_on_scalar(1, 2, 4)
+        store_rows(1, 2, 4)
+        relu_row_on_vector(2, 0)
+        relu_row_on_vector(2, 1)
+        relu_row_on_scalar(2, 2)
+        relu_row_on_scalar(2, 3)
+        square_rows_on_scalar(2, 0, 2)
+        store_rows(2, 0, 2)
         round_plain(vector, "out1", 0, T)
-        round_plain(vector, "out2", 0, HALF)
+        square_rows_on_vector(2, 3, 4)
+        square_rows_on_scalar(2, 2, 3)
+        store_rows(2, 2, 4)
         quantise("out1")
         store_codes(1)
-        round_plain(scalar, "out2", HALF, T)
+        round_plain(scalar, "out2", 304, T)
+        round_plain(vector, "out2", 0, 304)
         quantise("out2", 0, HALF)
         quantise("out2", HALF, T)
         store_codes(2)
         for r in range(4):
-            store_scales(nc.scalar if r % 2 else nc.sync, r)
+            store_scales(nc.scalar if r % 2 else nc.sync, r, 0, 3)

@@ -137,9 +137,9 @@ def tile_mix_linattn_fm_pl_relu2_kernel(tc, qc, kc, qd, st, vc_words, vc_scales,
 
         def h_decay(tb, partitions=P):
             nc.vector.tensor_tensor(
-                out=rounded["h"][:partitions, GROUP * tb : GROUP * (tb + 1)].rearrange("p (c i r) -> p c r i", i=PACK, r=PACK),
-                in0=h_bank[tb][:partitions, :].rearrange("p (r c i) -> p c r i", r=PACK, i=PACK),
-                in1=source("dm", tb * P, (tb + 1) * P)[:partitions].rearrange("p r (c i) -> p c r i", i=PACK),
+                out=rounded["h"][:partitions, GROUP * tb : GROUP * (tb + 1)].rearrange("p (c i r) -> p c r i", i=2, r=PACK),
+                in0=h_bank[tb][:partitions, :].rearrange("p (r c i) -> p c r i", r=PACK, i=2),
+                in1=source("dm", tb * P, (tb + 1) * P)[:partitions].rearrange("p r (c i) -> p c r i", i=2),
                 op=ALU.mult,
             )
 
@@ -228,8 +228,8 @@ def tile_mix_linattn_fm_pl_relu2_kernel(tc, qc, kc, qd, st, vc_words, vc_scales,
         load("kc", 0, T)
         load_vc_scales()
         load("qc", 0, T)
-        load("dm", 0, T)
         load("st0", 0, T)
+        load("dm", 0, T)
         load("qd", 0, HALF)
         load("qd", HALF, T)
         for a in range(1, GROUPS):
@@ -237,19 +237,20 @@ def tile_mix_linattn_fm_pl_relu2_kernel(tc, qc, kc, qd, st, vc_words, vc_scales,
             load(states[a], 0, T)
 
         deal_vc_words(0)
-        round_dealt(scalar, "kc", HALF, T)
-        round_dealt(vector, "kc", 0, HALF)
+        round_dealt(scalar, "kc", Q3, T)
+        round_dealt(vector, "kc", 0, Q3)
         deal_vc_scales(0)
-        deal_vc_scales(1)
         quantise("kc")
-        deal_vc_scales(2)
-        round_plain(scalar, "qc", P, HALF)
+        deal_vc_scales(1)
         round_plain(scalar, "qc", Q3, T)
-        round_plain(vector, "qc", 0, P)
-        round_plain(vector, "qc", Q2, Q3)
+        round_plain(vector, "qc", 0, Q3)
+        deal_vc_scales(2)
+        quantise("qc")
         for tb in range(4):
-            quantise("qc", tb * P, (tb + 1) * P)
             h_sums(tb, tb)
+        round_dealt(scalar, "st0", Q3, T)
+        round_dealt(vector, "st0", 0, Q3)
+        quantise("st0")
 
         def h_done(tb):
             quantise("h", tb * P, (tb + 1) * P)
@@ -259,75 +260,76 @@ def tile_mix_linattn_fm_pl_relu2_kernel(tc, qc, kc, qd, st, vc_words, vc_scales,
         h_decay(0)
         h_decay(1)
         h_done(0)
-        h_decay(2)
-        h_done(1)
-        round_dealt(scalar, "st0", HALF, T)
-        round_dealt(vector, "st0", 0, HALF)
-        h_done(2)
-        h_decay(3)
-        quantise("st0")
-        round_plain(scalar, "qd", 0, P)
         round_plain(scalar, "qd", P, HALF)
-        round_plain(scalar, "qd", Q2, Q3)
+        round_plain(scalar, "qd", Q3, T)
+        round_plain(vector, "qd", 0, P)
+        h_done(1)
         quantise("qd", 0, P)
         y_state(0, 0, False)
-        h_done(3)
         quantise("qd", P, HALF)
         y_state(0, 1, False)
-        round_plain(vector, "qd", Q3, T)
-        quantise("qd", Q2, Q3)
+        h_decay(2)
+        h_decay(3)
+        round_plain(vector, "qd", Q2, Q3)
+        quantise("h", HALF, T)
+        for tb in range(2, 4):
+            y_open(0, tb, 4 + tb)
+            y_values(0, tb, True)
+        quantise("qd", HALF, T)
         y_state(0, 2, False)
-        quantise("qd", Q3, T)
         y_state(0, 3, False)
         deal_vc_words(1)
         for r in range(PACK):
             rows_open(1, r, r)
         relu_on_scalar(0, 0)
         relu_on_scalar(0, 1)
-        square_on_vector(0, 0, P)
-        square_on_vector(0, P, HALF)
+        square_on_scalar(0, 0, HALF)
         store_out(0, 0, HALF)
         relu_on_scalar(0, 2)
         relu_on_scalar(0, 3)
-        square_on_scalar(0, HALF, T)
-        store_out(0, HALF, T)
         round_dealt(vector, "st1", 0, T)
         deal_vc_words(2)
         quantise("st1")
+        square_on_scalar(0, HALF, T)
+        store_out(0, HALF, T)
         for r in range(PACK):
             rows_close(1, r)
         for r in range(PACK):
             rows_open(2, r, 4 + r)
-        round_plain(scalar, "out0", 0, HALF)
-        round_plain(vector, "out0", HALF, T)
+        round_plain(vector, "out0", 0, HALF)
         round_dealt(vector, "st2", 0, T)
-        quantise("out0")
-        store_codes(0)
+        quantise("out0", 0, HALF)
         quantise("st2")
         for r in range(PACK):
             rows_close(2, r)
-        for r in range(PACK):
+        for r in range(3):
             relu_row_on_scalar(1, r)
-        square_rows_on_vector(1, 0, 2)
+        square_rows_on_scalar(1, 0, 2)
         store_rows(1, 0, 2)
-        square_rows_on_scalar(1, 2, 4)
+        relu_row_on_vector(1, 3)
+        round_plain(vector, "out0", HALF, T)
+        square_rows_on_vector(1, 2, 4)
         store_rows(1, 2, 4)
-        relu_row_on_vector(2, 0)
-        relu_row_on_vector(2, 1)
-        relu_row_on_scalar(2, 2)
-        relu_row_on_scalar(2, 3)
+        quantise("out0", HALF, T)
+        store_codes(0)
+        for r in range(3):
+            relu_row_on_scalar(2, r)
         square_rows_on_scalar(2, 0, 2)
         store_rows(2, 0, 2)
-        round_plain(vector, "out1", 0, T)
-        square_rows_on_vector(2, 3, 4)
-        square_rows_on_scalar(2, 2, 3)
+        relu_row_on_vector(2, 3)
+        square_rows_on_scalar(2, 2, 4)
         store_rows(2, 2, 4)
-        quantise("out1")
+        round_plain(vector, "out1", 0, HALF)
+        round_plain(vector, "out1", HALF, T)
+        quantise("out1", 0, HALF)
+        quantise("out1", HALF, T)
         store_codes(1)
-        round_plain(scalar, "out2", 304, T)
-        round_plain(vector, "out2", 0, 304)
+        round_plain(scalar, "out2", 384, T)
+        round_plain(vector, "out2", 0, HALF)
+        round_plain(vector, "out2", HALF, 384)
         quantise("out2", 0, HALF)
+        store_codes(2, 0, HALF)
         quantise("out2", HALF, T)
-        store_codes(2)
+        store_codes(2, HALF, T)
         for r in range(4):
             store_scales(nc.scalar if r % 2 else nc.sync, r, 0, 3)

@@ -43,8 +43,8 @@ def tile_mix_linattn_fm_pl_relu2_kernel(tc, qc, kc, qd, st, vc_words, vc_scales,
         def four_rows(dram):
             return dram.rearrange("(p j) w -> p j w", j=PACK)
 
-        vc_words_raw = [tile("vc_words_raw%d" % a, [P, GROUP], U16) for a in range(GROUPS)]
-        vc_words_dealt = [tile("vc_words_dealt%d" % a, [P, GROUP], U16) for a in range(GROUPS)]
+        vc_words_raw = tile("vc_words_raw", [P, M], U16)
+        vc_words_dealt = tile("vc_words_dealt", [P, M], U16)
         vc_scales_raw = tile("vc_scales_raw", [P, M], U8)
         vc_scales_dealt = tile("vc_scales_dealt", [P, M], U8)
         states = ["st%d" % a for a in range(GROUPS)]
@@ -74,17 +74,18 @@ def tile_mix_linattn_fm_pl_relu2_kernel(tc, qc, kc, qd, st, vc_words, vc_scales,
             pieces[name].append((c0, piece))
             nc.sync.dma_start(out=piece[:partitions], in_=four_rows(dram[name][:, c0:c1])[:partitions])
 
-        def load_vc_words(a):
-            nc.sync.dma_start(out=vc_words_raw[a][:].bitcast(I32), in_=vc_words[0][:, 2 * GROUP * a : 2 * GROUP * (a + 1)].bitcast(I32))
+        def load_vc_words(a0, a1):
+            nc.sync.dma_start(out=vc_words_raw[:, a0 * GROUP : a1 * GROUP].bitcast(I32), in_=vc_words[0][:, 2 * GROUP * a0 : 2 * GROUP * a1].bitcast(I32))
 
         def load_vc_scales():
             for r in range(4):
                 nc.sync.dma_start(out=vc_scales_raw[r:P:QUADRANT, :].bitcast(I32), in_=vc_scales[0, r:16:4, :].bitcast(I32))
 
-        def deal_vc_words(a):
-            nc.vector.tensor_copy(
-                out=vc_words_dealt[a][:].rearrange("p (r m) -> p m r", r=PACK),
-                in_=vc_words_raw[a][:].rearrange("p (m r) -> p m r", r=PACK),
+        def deal_vc_words(copy, a):
+            span = slice(a * GROUP, (a + 1) * GROUP)
+            copy(
+                out=vc_words_dealt[:, span].rearrange("p (r m) -> p m r", r=PACK),
+                in_=vc_words_raw[:, span].rearrange("p (m r) -> p m r", r=PACK),
             )
 
         def deal_vc_scales(a):
@@ -98,6 +99,12 @@ def tile_mix_linattn_fm_pl_relu2_kernel(tc, qc, kc, qd, st, vc_words, vc_scales,
             copy(
                 out=rounded[name][:].rearrange("p (r m j) -> p m j r", r=PACK, j=PACK)[:, c0 // PACK : c1 // PACK],
                 in_=source(name, c0, c1).rearrange("p j (m r) -> p m j r", r=PACK),
+            )
+
+        def round_runs(copy, name, r0, r1):
+            copy(
+                out=rounded[name][:].rearrange("p (r m j) -> p m j r", r=PACK, j=PACK)[:, :, :, r0:r1],
+                in_=source(name, 0, T).rearrange("p j (m r) -> p m j r", r=PACK)[:, :, :, r0:r1],
             )
 
         def round_plain(copy, name, c0, c1):
@@ -150,7 +157,7 @@ def tile_mix_linattn_fm_pl_relu2_kernel(tc, qc, kc, qd, st, vc_words, vc_scales,
             for r in range(PACK):
                 run = slice(r * P, (r + 1) * P)
                 col = a * GROUP + r * P
-                mx_pass(y_bank[a, tb][:, run], vc_words_dealt[a][:, run].bitcast(U8).bitcast(FP4X4), vc_scales_dealt[:, col : col + P], "h", tb, first and r == 0, not first and r == PACK - 1)
+                mx_pass(y_bank[a, tb][:, run], vc_words_dealt[:, col : col + P].bitcast(U8).bitcast(FP4X4), vc_scales_dealt[:, col : col + P], "h", tb, first and r == 0, not first and r == PACK - 1)
 
         def y_state(a, tb, first):
             for r in range(PACK):
@@ -163,7 +170,7 @@ def tile_mix_linattn_fm_pl_relu2_kernel(tc, qc, kc, qd, st, vc_words, vc_scales,
             col = a * GROUP + r * P
             nc.tensor.matmul_mx(
                 out=y_bank[a, r][:],
-                lhsT=vc_words_dealt[a][:, run].bitcast(U8).bitcast(FP4X4),
+                lhsT=vc_words_dealt[:, col : col + P].bitcast(U8).bitcast(FP4X4),
                 lhsT_scale=vc_scales_dealt[:, col : col + P],
                 rhs=codes["h"][:].bitcast(FP8X4),
                 rhs_scale=scales["h"],
@@ -195,6 +202,12 @@ def tile_mix_linattn_fm_pl_relu2_kernel(tc, qc, kc, qd, st, vc_words, vc_scales,
         def square_rows_on_vector(a, r0, r1):
             nc.vector.tensor_tensor(out=source(outs[a], 0, T)[:, r0:r1, :], in0=relu[a][:, r0:r1, :], in1=relu[a][:, r0:r1, :], op=ALU.mult)
 
+        def square_part_on_scalar(a, r0, r1, c0, c1):
+            nc.scalar.activation(out=source(outs[a], 0, T)[:, r0:r1, c0:c1], in_=relu[a][:, r0:r1, c0:c1], func=ACT.Square)
+
+        def square_part_on_vector(a, r0, r1, c0, c1):
+            nc.vector.tensor_tensor(out=source(outs[a], 0, T)[:, r0:r1, c0:c1], in0=relu[a][:, r0:r1, c0:c1], in1=relu[a][:, r0:r1, c0:c1], op=ALU.mult)
+
         def store_rows(a, r0, r1):
             nc.sync.dma_start(out=four_rows(out_0[a * GROUP : (a + 1) * GROUP, :])[:, r0:r1, :], in_=source(outs[a], 0, T)[:, r0:r1, :])
 
@@ -222,9 +235,19 @@ def tile_mix_linattn_fm_pl_relu2_kernel(tc, qc, kc, qd, st, vc_words, vc_scales,
                 in_=out_scales[r:P:QUADRANT, a0:a1].bitcast(I32),
             )
 
+
+        def state_ready(a, hf):
+            quantise(states[a], hf * HALF, (hf + 1) * HALF)
+            rows_close(a, 2 * hf)
+            rows_close(a, 2 * hf + 1)
+
+        def square_and_store(a, r):
+            square_rows_on_scalar(a, r, r + 1)
+            store_rows(a, r, r + 1)
+
         nc.vector.memset(vc_scales_raw[:].bitcast(I32), 0)
         Q2, Q3 = 2 * P, 3 * P
-        load_vc_words(0)
+        load_vc_words(0, 1)
         load("kc", 0, T)
         load_vc_scales()
         load("qc", 0, T)
@@ -233,10 +256,10 @@ def tile_mix_linattn_fm_pl_relu2_kernel(tc, qc, kc, qd, st, vc_words, vc_scales,
         load("qd", 0, HALF)
         load("qd", HALF, T)
         for a in range(1, GROUPS):
-            load_vc_words(a)
+            load_vc_words(a, a + 1)
             load(states[a], 0, T)
 
-        deal_vc_words(0)
+        deal_vc_words(vector, 0)
         round_dealt(scalar, "kc", Q3, T)
         round_dealt(vector, "kc", 0, Q3)
         deal_vc_scales(0)
@@ -272,61 +295,60 @@ def tile_mix_linattn_fm_pl_relu2_kernel(tc, qc, kc, qd, st, vc_words, vc_scales,
         h_decay(3)
         round_plain(vector, "qd", Q2, Q3)
         quantise("h", HALF, T)
+        quantise("qd", HALF, T)
         for tb in range(2, 4):
             y_open(0, tb, 4 + tb)
             y_values(0, tb, True)
-        quantise("qd", HALF, T)
-        y_state(0, 2, False)
-        y_state(0, 3, False)
-        deal_vc_words(1)
+            y_state(0, tb, False)
+        deal_vc_words(vector, 1)
         for r in range(PACK):
             rows_open(1, r, r)
-        relu_on_scalar(0, 0)
-        relu_on_scalar(0, 1)
-        square_on_scalar(0, 0, HALF)
-        store_out(0, 0, HALF)
-        relu_on_scalar(0, 2)
-        relu_on_scalar(0, 3)
+        for hf in range(2):
+            relu_on_scalar(0, 2 * hf)
+            relu_on_scalar(0, 2 * hf + 1)
+            square_on_scalar(0, 2 * hf * P, (2 * hf + 1) * P)
+            square_on_scalar(0, (2 * hf + 1) * P, (2 * hf + 2) * P)
+            store_out(0, hf * HALF, (hf + 1) * HALF)
         round_dealt(vector, "st1", 0, T)
-        deal_vc_words(2)
-        quantise("st1")
-        square_on_scalar(0, HALF, T)
-        store_out(0, HALF, T)
-        for r in range(PACK):
-            rows_close(1, r)
+        deal_vc_words(vector, 2)
+        state_ready(1, 0)
+        state_ready(1, 1)
+        round_plain(vector, "out0", 0, HALF)
         for r in range(PACK):
             rows_open(2, r, 4 + r)
-        round_plain(vector, "out0", 0, HALF)
         round_dealt(vector, "st2", 0, T)
         quantise("out0", 0, HALF)
-        quantise("st2")
-        for r in range(PACK):
-            rows_close(2, r)
-        for r in range(3):
-            relu_row_on_scalar(1, r)
-        square_rows_on_scalar(1, 0, 2)
-        store_rows(1, 0, 2)
-        relu_row_on_vector(1, 3)
+        store_codes(0, 0, HALF)
+        state_ready(2, 0)
+        relu_row_on_scalar(1, 0)
+        relu_row_on_scalar(1, 1)
+        square_and_store(1, 0)
+        square_and_store(1, 1)
+        relu_row_on_vector(1, 2)
+        state_ready(2, 1)
+        relu_row_on_scalar(1, 3)
+        square_and_store(1, 2)
+        square_and_store(1, 3)
         round_plain(vector, "out0", HALF, T)
-        square_rows_on_vector(1, 2, 4)
-        store_rows(1, 2, 4)
+        relu_row_on_vector(2, 0)
         quantise("out0", HALF, T)
-        store_codes(0)
-        for r in range(3):
-            relu_row_on_scalar(2, r)
-        square_rows_on_scalar(2, 0, 2)
-        store_rows(2, 0, 2)
+        store_codes(0, HALF, T)
+        relu_row_on_scalar(2, 1)
+        relu_row_on_vector(2, 2)
         relu_row_on_vector(2, 3)
-        square_rows_on_scalar(2, 2, 4)
-        store_rows(2, 2, 4)
+        square_and_store(2, 0)
+        square_and_store(2, 1)
         round_plain(vector, "out1", 0, HALF)
         round_plain(vector, "out1", HALF, T)
         quantise("out1", 0, HALF)
         quantise("out1", HALF, T)
+        square_part_on_scalar(2, 2, 4, 0, HALF)
+        square_part_on_scalar(2, 2, 4, HALF, T)
+        store_rows(2, 2, 4)
         store_codes(1)
-        round_plain(scalar, "out2", 384, T)
+        round_plain(scalar, "out2", Q3, T)
         round_plain(vector, "out2", 0, HALF)
-        round_plain(vector, "out2", HALF, 384)
+        round_plain(vector, "out2", HALF, Q3)
         quantise("out2", 0, HALF)
         store_codes(2, 0, HALF)
         quantise("out2", HALF, T)

@@ -107,9 +107,16 @@ def tile_mix_linattn_fm_pl_relu2_kernel(tc, qc, kc, qd, st, vc_words, vc_scales,
                 in_=source(name, 0, T).rearrange("p j (m r) -> p m j r", r=PACK)[:, :, :, r0:r1],
             )
 
+        def gpsimd(out, in_):
+            nc.gpsimd.tensor_scalar(out=out, in0=in_, scalar1=1.0, scalar2=0.0, op0=ALU.mult, op1=ALU.add)
+
+        def rounded_columns(name, c0, c1):
+            holder = states[-1] if name == outs[0] and c0 >= HALF else name
+            return rounded[holder][:, PACK * c0 : PACK * c1]
+
         def round_plain(copy, name, c0, c1):
             copy(
-                out=rounded[name][:, PACK * c0 : PACK * c1].rearrange("p (c i j) -> p c j i", i=PACK, j=PACK),
+                out=rounded_columns(name, c0, c1).rearrange("p (c i j) -> p c j i", i=PACK, j=PACK),
                 in_=source(name, c0, c1).rearrange("p j (c i) -> p c j i", i=PACK),
             )
 
@@ -117,7 +124,7 @@ def tile_mix_linattn_fm_pl_relu2_kernel(tc, qc, kc, qd, st, vc_words, vc_scales,
             nc.vector.quantize_mx(
                 out=codes[name][:, c0:c1].bitcast(FP8X4),
                 scales=scales[name][:, c0:c1],
-                in_=rounded[name][:, PACK * c0 : PACK * c1],
+                in_=rounded_columns(name, c0, c1),
             )
 
         def quantise_keys(hf):
@@ -287,11 +294,11 @@ def tile_mix_linattn_fm_pl_relu2_kernel(tc, qc, kc, qd, st, vc_words, vc_scales,
         round_plain(scalar, "qd", Q3, T)
         round_plain(vector, "qd", 0, P)
         h_done(1)
+        h_decay(2)
         quantise("qd", 0, P)
         y_state(0, 0, False)
         quantise("qd", P, HALF)
         y_state(0, 1, False)
-        h_decay(2)
         h_decay(3)
         round_plain(vector, "qd", Q2, Q3)
         quantise("h", HALF, T)
@@ -320,22 +327,22 @@ def tile_mix_linattn_fm_pl_relu2_kernel(tc, qc, kc, qd, st, vc_words, vc_scales,
         quantise("out0", 0, HALF)
         store_codes(0, 0, HALF)
         state_ready(2, 0)
+        state_ready(2, 1)
+        round_plain(gpsimd, "out0", HALF, T)
         relu_row_on_scalar(1, 0)
         relu_row_on_scalar(1, 1)
         square_and_store(1, 0)
+        relu_row_on_scalar(1, 2)
         square_and_store(1, 1)
-        relu_row_on_vector(1, 2)
-        state_ready(2, 1)
-        relu_row_on_scalar(1, 3)
+        relu_row_on_vector(1, 3)
         square_and_store(1, 2)
         square_and_store(1, 3)
-        round_plain(vector, "out0", HALF, T)
         relu_row_on_vector(2, 0)
-        quantise("out0", HALF, T)
-        store_codes(0, HALF, T)
         relu_row_on_scalar(2, 1)
         relu_row_on_vector(2, 2)
         relu_row_on_vector(2, 3)
+        quantise("out0", HALF, T)
+        store_codes(0, HALF, T)
         square_and_store(2, 0)
         square_and_store(2, 1)
         round_plain(vector, "out1", 0, HALF)
@@ -343,11 +350,11 @@ def tile_mix_linattn_fm_pl_relu2_kernel(tc, qc, kc, qd, st, vc_words, vc_scales,
         quantise("out1", 0, HALF)
         quantise("out1", HALF, T)
         square_part_on_scalar(2, 2, 4, 0, HALF)
+        round_plain(vector, "out2", 0, HALF)
         square_part_on_scalar(2, 2, 4, HALF, T)
         store_rows(2, 2, 4)
         store_codes(1)
         round_plain(scalar, "out2", Q3, T)
-        round_plain(vector, "out2", 0, HALF)
         round_plain(vector, "out2", HALF, Q3)
         quantise("out2", 0, HALF)
         store_codes(2, 0, HALF)

@@ -338,7 +338,7 @@ def tile_mix_linattn_fm_pl_relu2_kernel(tc, qc, kc, qd, st, vc_words, vc_scales,
         square_and_store(1, 2)
         square_and_store(1, 3)
         relu_row_on_vector(2, 0)
-        relu_row_on_scalar(2, 1)
+        relu_row_on_vector(2, 1)
         relu_row_on_vector(2, 2)
         relu_row_on_vector(2, 3)
         quantise("out0", HALF, T)

@@ -20,10 +20,8 @@ P = 128
 PACK = 4
 GROUP = P * PACK
 GROUPS = M // GROUP
-BANKS = 8
 QUADRANT = 32
 HALF = T // 2
-RUN = P // 2
 
 
 def tile_mix_linattn_fm_pl_relu2_kernel(tc, qc, kc, qd, st, vc_words, vc_scales, dm, out_0, out_1, out_2):
@@ -43,8 +41,8 @@ def tile_mix_linattn_fm_pl_relu2_kernel(tc, qc, kc, qd, st, vc_words, vc_scales,
         def four_rows(dram):
             return dram.rearrange("(p j) w -> p j w", j=PACK)
 
-        vc_words_raw = tile("vc_words_raw", [P, M], U16)
-        vc_words_dealt = tile("vc_words_dealt", [P, M], U16)
+        words_raw = {}
+        words = [tile("words%d" % a, [P, GROUP], U16) for a in range(GROUPS)]
         vc_scales_raw = tile("vc_scales_raw", [P, M], U8)
         vc_scales_dealt = tile("vc_scales_dealt", [P, M], U8)
         states = ["st%d" % a for a in range(GROUPS)]
@@ -69,33 +67,32 @@ def tile_mix_linattn_fm_pl_relu2_kernel(tc, qc, kc, qd, st, vc_words, vc_scales,
             first, piece = [entry for entry in pieces[name] if entry[0] <= c0][-1]
             return piece[:, :, c0 - first : c1 - first]
 
-        def load(name, c0, c1, partitions=P):
+        def load(name, c0=0, c1=T):
             piece = tile("%s_%d_f32" % (name, c0), [P, PACK, c1 - c0], F32)
             pieces[name].append((c0, piece))
-            nc.sync.dma_start(out=piece[:partitions], in_=four_rows(dram[name][:, c0:c1])[:partitions])
+            nc.sync.dma_start(out=piece[:], in_=four_rows(dram[name][:, c0:c1]))
 
-        def load_vc_words(a0, a1):
-            nc.sync.dma_start(out=vc_words_raw[:, a0 * GROUP : a1 * GROUP].bitcast(I32), in_=vc_words[0][:, 2 * GROUP * a0 : 2 * GROUP * a1].bitcast(I32))
+        def load_words(a0, a1):
+            piece = tile("words_raw%d" % a0, [P, GROUP * (a1 - a0)], U16)
+            for a in range(a0, a1):
+                words_raw[a] = piece[:, (a - a0) * GROUP : (a - a0 + 1) * GROUP]
+            nc.sync.dma_start(out=piece[:].bitcast(I32), in_=vc_words[0][:, 2 * GROUP * a0 : 2 * GROUP * a1].bitcast(I32))
 
         def load_vc_scales():
             for r in range(4):
                 nc.sync.dma_start(out=vc_scales_raw[r:P:QUADRANT, :].bitcast(I32), in_=vc_scales[0, r:16:4, :].bitcast(I32))
 
-        def deal_vc_words(copy, a):
-            span = slice(a * GROUP, (a + 1) * GROUP)
-            copy(
-                out=vc_words_dealt[:, span].rearrange("p (r m) -> p m r", r=PACK),
-                in_=vc_words_raw[:, span].rearrange("p (m r) -> p m r", r=PACK),
-            )
+        def deal_words(copy, a):
+            copy(out=words[a][:].rearrange("p (r m) -> p m r", r=PACK), in_=words_raw[a].rearrange("p (m r) -> p m r", r=PACK))
 
-        def deal_vc_scales(a):
+        def deal_scales(a):
             span = slice(a * GROUP, (a + 1) * GROUP)
             nc.vector.tensor_copy(
                 out=vc_scales_dealt[:, span].rearrange("p (r m) -> p r m", r=PACK),
                 in_=vc_scales_raw[:, span].rearrange("p (m r) -> p r m", r=PACK),
             )
 
-        def round_dealt(copy, name, c0, c1):
+        def round_dealt(copy, name, c0=0, c1=T):
             copy(
                 out=rounded[name][:].rearrange("p (r m j) -> p m j r", r=PACK, j=PACK)[:, c0 // PACK : c1 // PACK],
                 in_=source(name, c0, c1).rearrange("p j (m r) -> p m j r", r=PACK),
@@ -107,131 +104,84 @@ def tile_mix_linattn_fm_pl_relu2_kernel(tc, qc, kc, qd, st, vc_words, vc_scales,
                 in_=source(name, 0, T).rearrange("p j (m r) -> p m j r", r=PACK)[:, :, :, r0:r1],
             )
 
-        def gpsimd(out, in_):
-            nc.gpsimd.tensor_scalar(out=out, in0=in_, scalar1=1.0, scalar2=0.0, op0=ALU.mult, op1=ALU.add)
-
-        def rounded_columns(name, c0, c1):
-            holder = states[-1] if name == outs[0] and c0 >= HALF else name
-            return rounded[holder][:, PACK * c0 : PACK * c1]
-
-        def round_plain(copy, name, c0, c1):
+        def round_plain(copy, name, c0=0, c1=T):
             copy(
-                out=rounded_columns(name, c0, c1).rearrange("p (c i j) -> p c j i", i=PACK, j=PACK),
+                out=rounded[name][:, PACK * c0 : PACK * c1].rearrange("p (c i j) -> p c j i", i=PACK, j=PACK),
                 in_=source(name, c0, c1).rearrange("p j (c i) -> p c j i", i=PACK),
             )
 
         def quantise(name, c0=0, c1=T):
-            nc.vector.quantize_mx(
-                out=codes[name][:, c0:c1].bitcast(FP8X4),
-                scales=scales[name][:, c0:c1],
-                in_=rounded_columns(name, c0, c1),
-            )
+            nc.vector.quantize_mx(out=codes[name][:, c0:c1].bitcast(FP8X4), scales=scales[name][:, c0:c1], in_=rounded[name][:, PACK * c0 : PACK * c1])
 
-        def quantise_keys(hf):
-            for r in range(PACK):
-                quantise("kc", r * P + hf * RUN, r * P + (hf + 1) * RUN)
-
-        def mx_pass(out, stationary, stationary_scale, name, tb, start, stop):
-            queries = slice(tb * P, (tb + 1) * P)
+        def mx_pass(out, stationary, stationary_scale, name, c0, c1, start, stop):
             nc.tensor.matmul_mx(
                 out=out,
                 lhsT=stationary,
                 lhsT_scale=stationary_scale,
-                rhs=codes[name][:, queries].bitcast(FP8X4),
-                rhs_scale=scales[name][:, queries],
+                rhs=codes[name][:, c0:c1].bitcast(FP8X4),
+                rhs_scale=scales[name][:, c0:c1],
                 start=start,
                 stop=stop,
             )
+
+        def values(a, r):
+            col = a * GROUP + r * P
+            return words[a][:, r * P : (r + 1) * P].bitcast(U8).bitcast(FP4X4), vc_scales_dealt[:, col : col + P]
+
+        def state(a, r):
+            run = slice(r * P, (r + 1) * P)
+            return codes[states[a]][:, run].bitcast(FP8X4), scales[states[a]][:, run]
 
         def h_sums(tb, number):
             h_bank[tb] = bank(number, "h_bank%d" % tb)
             for r in range(PACK):
                 run = slice(r * P, (r + 1) * P)
-                mx_pass(h_bank[tb][:, run], codes["kc"][:, run].bitcast(FP8X4), scales["kc"][:, run], "qc", tb, True, True)
+                mx_pass(h_bank[tb][:, run], codes["kc"][:, run].bitcast(FP8X4), scales["kc"][:, run], "qc", tb * P, (tb + 1) * P, True, True)
 
-        def h_decay(tb, partitions=P):
+        def h_decay(tb):
             nc.vector.tensor_tensor(
-                out=rounded["h"][:partitions, GROUP * tb : GROUP * (tb + 1)].rearrange("p (c i r) -> p c r i", i=2, r=PACK),
-                in0=h_bank[tb][:partitions, :].rearrange("p (r c i) -> p c r i", r=PACK, i=2),
-                in1=source("dm", tb * P, (tb + 1) * P)[:partitions].rearrange("p r (c i) -> p c r i", i=2),
+                out=rounded["h"][:, GROUP * tb : GROUP * (tb + 1)].rearrange("p (c i r) -> p c r i", i=2, r=PACK),
+                in0=h_bank[tb][:].rearrange("p (r c i) -> p c r i", r=PACK, i=2),
+                in1=source("dm", tb * P, (tb + 1) * P).rearrange("p r (c i) -> p c r i", i=2),
                 op=ALU.mult,
             )
 
-        def y_open(a, tb, number):
+        def block_open(a, tb, number):
             y_bank[a, tb] = bank(number, "y_bank%d%d" % (a, tb))
-
-        def y_values(a, tb, first):
             for r in range(PACK):
-                run = slice(r * P, (r + 1) * P)
-                col = a * GROUP + r * P
-                mx_pass(y_bank[a, tb][:, run], vc_words_dealt[:, col : col + P].bitcast(U8).bitcast(FP4X4), vc_scales_dealt[:, col : col + P], "h", tb, first and r == 0, not first and r == PACK - 1)
+                mx_pass(y_bank[a, tb][:, r * P : (r + 1) * P], *values(a, r), "h", tb * P, (tb + 1) * P, r == 0, False)
 
-        def y_state(a, tb, first):
+        def block_close(a, tb):
             for r in range(PACK):
-                run = slice(r * P, (r + 1) * P)
-                mx_pass(y_bank[a, tb][:, run], codes[states[a]][:, run].bitcast(FP8X4), scales[states[a]][:, run], "qd", tb, first and r == 0, not first and r == PACK - 1)
+                mx_pass(y_bank[a, tb][:, r * P : (r + 1) * P], *state(a, r), "qd", tb * P, (tb + 1) * P, False, r == PACK - 1)
 
-        def rows_open(a, r, number):
+        def row_open(a, r, number):
             y_bank[a, r] = bank(number, "y_bank%d%d" % (a, r))
-            run = slice(r * P, (r + 1) * P)
-            col = a * GROUP + r * P
-            nc.tensor.matmul_mx(
-                out=y_bank[a, r][:],
-                lhsT=vc_words_dealt[:, col : col + P].bitcast(U8).bitcast(FP4X4),
-                lhsT_scale=vc_scales_dealt[:, col : col + P],
-                rhs=codes["h"][:].bitcast(FP8X4),
-                rhs_scale=scales["h"],
-                start=True,
-                stop=False,
-            )
+            mx_pass(y_bank[a, r][:], *values(a, r), "h", 0, T, True, False)
 
-        def rows_close(a, r):
-            run = slice(r * P, (r + 1) * P)
-            nc.tensor.matmul_mx(
-                out=y_bank[a, r][:],
-                lhsT=codes[states[a]][:, run].bitcast(FP8X4),
-                lhsT_scale=scales[states[a]][:, run],
-                rhs=codes["qd"][:].bitcast(FP8X4),
-                rhs_scale=scales["qd"],
-                start=False,
-                stop=True,
-            )
+        def row_close(a, r):
+            mx_pass(y_bank[a, r][:], *state(a, r), "qd", 0, T, False, True)
 
-        def relu_row_on_scalar(a, r):
-            nc.scalar.activation(out=relu[a][:, r, :], in_=y_bank[a, r][:], func=ACT.Relu)
+        def relu_scalar(out, in_):
+            nc.scalar.activation(out=out, in_=in_, func=ACT.Relu)
 
-        def relu_row_on_vector(a, r):
-            nc.vector.tensor_scalar(out=relu[a][:, r, :], in0=y_bank[a, r][:], scalar1=0.0, scalar2=None, op0=ALU.max)
+        def relu_vector(out, in_):
+            nc.vector.tensor_scalar(out=out, in0=in_, scalar1=0.0, scalar2=None, op0=ALU.max)
 
-        def square_rows_on_scalar(a, r0, r1):
-            nc.scalar.activation(out=source(outs[a], 0, T)[:, r0:r1, :], in_=relu[a][:, r0:r1, :], func=ACT.Square)
+        def relu_block(engine, a, tb):
+            engine(relu[a][:, :, tb * P : (tb + 1) * P], y_bank[a, tb][:].rearrange("p (r t) -> p r t", r=PACK))
 
-        def square_rows_on_vector(a, r0, r1):
-            nc.vector.tensor_tensor(out=source(outs[a], 0, T)[:, r0:r1, :], in0=relu[a][:, r0:r1, :], in1=relu[a][:, r0:r1, :], op=ALU.mult)
+        def relu_row(engine, a, r):
+            engine(relu[a][:, r, :], y_bank[a, r][:])
 
-        def square_part_on_scalar(a, r0, r1, c0, c1):
+        def square(a, r0, r1, c0=0, c1=T):
             nc.scalar.activation(out=source(outs[a], 0, T)[:, r0:r1, c0:c1], in_=relu[a][:, r0:r1, c0:c1], func=ACT.Square)
 
-        def square_part_on_vector(a, r0, r1, c0, c1):
+        def square_vector(a, r0, r1, c0=0, c1=T):
             nc.vector.tensor_tensor(out=source(outs[a], 0, T)[:, r0:r1, c0:c1], in0=relu[a][:, r0:r1, c0:c1], in1=relu[a][:, r0:r1, c0:c1], op=ALU.mult)
 
-        def store_rows(a, r0, r1):
-            nc.sync.dma_start(out=four_rows(out_0[a * GROUP : (a + 1) * GROUP, :])[:, r0:r1, :], in_=source(outs[a], 0, T)[:, r0:r1, :])
-
-        def relu_on_scalar(a, tb):
-            nc.scalar.activation(out=relu[a][:, :, tb * P : (tb + 1) * P], in_=y_bank[a, tb][:].rearrange("p (r t) -> p r t", r=PACK), func=ACT.Relu)
-
-        def relu_on_vector(a, tb):
-            nc.vector.tensor_scalar(out=relu[a][:, :, tb * P : (tb + 1) * P], in0=y_bank[a, tb][:].rearrange("p (r t) -> p r t", r=PACK), scalar1=0.0, scalar2=None, op0=ALU.max)
-
-        def square_on_scalar(a, c0, c1):
-            nc.scalar.activation(out=source(outs[a], c0, c1), in_=relu[a][:, :, c0:c1], func=ACT.Square)
-
-        def square_on_vector(a, c0, c1):
-            nc.vector.tensor_tensor(out=source(outs[a], c0, c1), in0=relu[a][:, :, c0:c1], in1=relu[a][:, :, c0:c1], op=ALU.mult)
-
-        def store_out(a, c0, c1):
-            nc.sync.dma_start(out=four_rows(out_0[a * GROUP : (a + 1) * GROUP, c0:c1]), in_=source(outs[a], c0, c1))
+        def store_rows(a, r0, r1, c0=0, c1=T):
+            nc.sync.dma_start(out=four_rows(out_0[a * GROUP : (a + 1) * GROUP, c0:c1])[:, r0:r1, :], in_=source(outs[a], 0, T)[:, r0:r1, c0:c1])
 
         def store_codes(a, c0=0, c1=T):
             nc.sync.dma_start(out=out_1[a].rearrange("p t i -> p (t i)").bitcast(I32)[:, c0:c1], in_=codes[outs[a]][:, c0:c1].bitcast(I32))
@@ -242,120 +192,133 @@ def tile_mix_linattn_fm_pl_relu2_kernel(tc, qc, kc, qd, st, vc_words, vc_scales,
                 in_=out_scales[r:P:QUADRANT, a0:a1].bitcast(I32),
             )
 
-
-        def state_ready(a, hf):
-            quantise(states[a], hf * HALF, (hf + 1) * HALF)
-            rows_close(a, 2 * hf)
-            rows_close(a, 2 * hf + 1)
-
-        def square_and_store(a, r):
-            square_rows_on_scalar(a, r, r + 1)
-            store_rows(a, r, r + 1)
+        Q1, Q2, Q3 = P, 2 * P, 3 * P
 
         nc.vector.memset(vc_scales_raw[:].bitcast(I32), 0)
-        Q2, Q3 = 2 * P, 3 * P
-        load_vc_words(0, 1)
-        load("kc", 0, T)
+        load_words(0, 1)
+        load("kc")
         load_vc_scales()
-        load("qc", 0, T)
-        load("st0", 0, T)
-        load("dm", 0, T)
+        load("qc")
+        load("dm")
+        load("st0")
         load("qd", 0, HALF)
         load("qd", HALF, T)
-        for a in range(1, GROUPS):
-            load_vc_words(a, a + 1)
-            load(states[a], 0, T)
+        load_words(1, 2)
+        load("st1")
+        load_words(2, 3)
+        load("st2")
 
-        deal_vc_words(vector, 0)
+        deal_words(vector, 0)
         round_dealt(scalar, "kc", Q3, T)
         round_dealt(vector, "kc", 0, Q3)
-        deal_vc_scales(0)
+        deal_scales(0)
         quantise("kc")
-        deal_vc_scales(1)
+        deal_scales(1)
+        deal_scales(2)
         round_plain(scalar, "qc", Q3, T)
-        round_plain(vector, "qc", 0, Q3)
-        deal_vc_scales(2)
-        quantise("qc")
-        for tb in range(4):
-            h_sums(tb, tb)
-        round_dealt(scalar, "st0", Q3, T)
-        round_dealt(vector, "st0", 0, Q3)
-        quantise("st0")
-
-        def h_done(tb):
-            quantise("h", tb * P, (tb + 1) * P)
-            y_open(0, tb, 4 + tb)
-            y_values(0, tb, True)
-
+        round_plain(vector, "qc", 0, Q1)
+        round_plain(vector, "qc", Q1, Q2)
+        quantise("qc", 0, Q1)
+        h_sums(0, 0)
+        round_plain(vector, "qc", Q2, Q3)
+        quantise("qc", Q1, Q2)
+        h_sums(1, 1)
+        quantise("qc", Q2, T)
+        h_sums(2, 2)
+        h_sums(3, 3)
         h_decay(0)
         h_decay(1)
-        h_done(0)
-        round_plain(scalar, "qd", P, HALF)
-        round_plain(scalar, "qd", Q3, T)
-        round_plain(vector, "qd", 0, P)
-        h_done(1)
         h_decay(2)
-        quantise("qd", 0, P)
-        y_state(0, 0, False)
-        quantise("qd", P, HALF)
-        y_state(0, 1, False)
+        quantise("h", 0, HALF)
         h_decay(3)
-        round_plain(vector, "qd", Q2, Q3)
+        block_open(0, 0, 4)
+        block_open(0, 1, 5)
+        round_dealt(scalar, "st0", 320, T)
+        round_dealt(vector, "st0", 0, 320)
         quantise("h", HALF, T)
-        quantise("qd", HALF, T)
-        for tb in range(2, 4):
-            y_open(0, tb, 4 + tb)
-            y_values(0, tb, True)
-            y_state(0, tb, False)
-        deal_vc_words(vector, 1)
+        block_open(0, 2, 6)
+        block_open(0, 3, 7)
+        quantise("st0")
+        round_plain(scalar, "qd", 0, Q1)
+        round_plain(vector, "qd", Q1, Q2)
+        quantise("qd", 0, Q1)
+        block_close(0, 0)
+        quantise("qd", Q1, Q2)
+        block_close(0, 1)
+        round_plain(vector, "qd", Q2, Q3)
+        round_plain(scalar, "qd", Q3, T)
+        deal_words(vector, 1)
+        quantise("qd", Q2, Q3)
+        block_close(0, 2)
+        quantise("qd", Q3, T)
+        block_close(0, 3)
+
         for r in range(PACK):
-            rows_open(1, r, r)
-        for hf in range(2):
-            relu_on_scalar(0, 2 * hf)
-            relu_on_scalar(0, 2 * hf + 1)
-            square_on_scalar(0, 2 * hf * P, (2 * hf + 1) * P)
-            square_on_scalar(0, (2 * hf + 1) * P, (2 * hf + 2) * P)
-            store_out(0, hf * HALF, (hf + 1) * HALF)
-        round_dealt(vector, "st1", 0, T)
-        deal_vc_words(vector, 2)
-        state_ready(1, 0)
-        state_ready(1, 1)
-        round_plain(vector, "out0", 0, HALF)
-        for r in range(PACK):
-            rows_open(2, r, 4 + r)
-        round_dealt(vector, "st2", 0, T)
+            row_open(1, r, r)
+        relu_block(relu_scalar, 0, 0)
+        relu_block(relu_vector, 0, 1)
+        square(0, 0, 4, 0, Q1)
+        square_vector(0, 0, 4, Q1, Q2)
+        round_plain(vector, "out0", 0, Q1)
+        relu_block(relu_scalar, 0, 2)
+        relu_block(relu_scalar, 0, 3)
+        square(0, 0, 4, Q2, Q3)
+        square(0, 0, 4, Q3, T)
+        store_rows(0, 0, 4)
+        round_runs(vector, "st1", 0, 2)
+        deal_words(vector, 2)
+        quantise("st1", 0, HALF)
+        row_close(1, 0)
+        row_close(1, 1)
+        row_open(2, 0, 4)
+        row_open(2, 1, 5)
+        round_runs(vector, "st1", 2, 4)
+        round_plain(vector, "out0", Q1, Q2)
+        quantise("st1", HALF, T)
+        row_close(1, 2)
+        row_close(1, 3)
+        row_open(2, 2, 6)
+        row_open(2, 3, 7)
+        round_plain(scalar, "out0", Q2, Q3)
+        round_runs(vector, "st2", 0, 2)
+        round_plain(vector, "out0", Q3, T)
+        quantise("st2", 0, HALF)
+        row_close(2, 0)
+        row_close(2, 1)
+        round_runs(vector, "st2", 2, 4)
         quantise("out0", 0, HALF)
-        store_codes(0, 0, HALF)
-        state_ready(2, 0)
-        state_ready(2, 1)
-        round_plain(gpsimd, "out0", HALF, T)
-        relu_row_on_scalar(1, 0)
-        relu_row_on_scalar(1, 1)
-        square_and_store(1, 0)
-        relu_row_on_scalar(1, 2)
-        square_and_store(1, 1)
-        relu_row_on_vector(1, 3)
-        square_and_store(1, 2)
-        square_and_store(1, 3)
-        relu_row_on_vector(2, 0)
-        relu_row_on_vector(2, 1)
-        relu_row_on_vector(2, 2)
-        relu_row_on_vector(2, 3)
+        quantise("st2", HALF, T)
+        row_close(2, 2)
+        row_close(2, 3)
         quantise("out0", HALF, T)
-        store_codes(0, HALF, T)
-        square_and_store(2, 0)
-        square_and_store(2, 1)
-        round_plain(vector, "out1", 0, HALF)
-        round_plain(vector, "out1", HALF, T)
-        quantise("out1", 0, HALF)
-        quantise("out1", HALF, T)
-        square_part_on_scalar(2, 2, 4, 0, HALF)
-        round_plain(vector, "out2", 0, HALF)
-        square_part_on_scalar(2, 2, 4, HALF, T)
-        store_rows(2, 2, 4)
-        store_codes(1)
+        relu_row(relu_scalar, 1, 0)
+        relu_row(relu_scalar, 1, 1)
+        square(1, 0, 1)
+        store_rows(1, 0, 1)
+        square(1, 1, 2)
+        store_rows(1, 1, 2)
+        store_codes(0)
+        relu_row(relu_scalar, 1, 2)
+        relu_row(relu_scalar, 1, 3)
+        square(1, 2, 3)
+        store_rows(1, 2, 3)
+        square(1, 3, 4)
+        store_rows(1, 3, 4)
+        for r in range(PACK):
+            relu_row(relu_vector, 2, r)
+        for r in range(3):
+            square(2, r, r + 1)
+            store_rows(2, r, r + 1)
+        square(2, 3, 4, 0, HALF)
+        square(2, 3, 4, HALF, T)
+        store_rows(2, 3, 4)
+        round_plain(vector, "out1")
+        round_plain(scalar, "out2", 0, Q1)
         round_plain(scalar, "out2", Q3, T)
-        round_plain(vector, "out2", HALF, Q3)
+        round_plain(vector, "out2", Q1, Q2)
+        quantise("out1")
+        store_codes(1)
+        round_plain(vector, "out2", Q2, Q3)
         quantise("out2", 0, HALF)
         store_codes(2, 0, HALF)
         quantise("out2", HALF, T)

@@ -83,7 +83,7 @@ def tile_mix_linattn_fm_pl_relu2_kernel(tc, qc, kc, qd, st, vc_words, vc_scales,
                 nc.sync.dma_start(out=vc_scales_raw[r:P:QUADRANT, :].bitcast(I32), in_=vc_scales[0, r:16:4, :].bitcast(I32))
 
         def deal_words(copy, a):
-            copy(out=words[a][:].rearrange("p (r m) -> p m r", r=PACK), in_=words_raw[a].rearrange("p (m r) -> p m r", r=PACK))
+            copy(out=words[a][:].rearrange("p (r m) -> p r m", r=PACK), in_=words_raw[a].rearrange("p (m r) -> p r m", r=PACK))
 
         def deal_scales(a):
             span = slice(a * GROUP, (a + 1) * GROUP)
@@ -94,8 +94,8 @@ def tile_mix_linattn_fm_pl_relu2_kernel(tc, qc, kc, qd, st, vc_words, vc_scales,
 
         def round_dealt(copy, name, c0=0, c1=T):
             copy(
-                out=rounded[name][:].rearrange("p (r m j) -> p m j r", r=PACK, j=PACK)[:, c0 // PACK : c1 // PACK],
-                in_=source(name, c0, c1).rearrange("p j (m r) -> p m j r", r=PACK),
+                out=rounded[name][:].rearrange("p (s r m j) -> p s m j r", s=2, r=2, j=PACK)[:, :, c0 // PACK : c1 // PACK],
+                in_=source(name, c0, c1).rearrange("p j (m s r) -> p s m j r", s=2, r=2),
             )
 
         def round_runs(copy, name, r0, r1):
@@ -106,8 +106,8 @@ def tile_mix_linattn_fm_pl_relu2_kernel(tc, qc, kc, qd, st, vc_words, vc_scales,
 
         def round_plain(copy, name, c0=0, c1=T):
             copy(
-                out=rounded[name][:, PACK * c0 : PACK * c1].rearrange("p (c i j) -> p c j i", i=PACK, j=PACK),
-                in_=source(name, c0, c1).rearrange("p j (c i) -> p c j i", i=PACK),
+                out=rounded[name][:, PACK * c0 : PACK * c1].rearrange("p (c i j) -> p c j i", i=2, j=PACK),
+                in_=source(name, c0, c1).rearrange("p j (c i) -> p c j i", i=2),
             )
 
         def quantise(name, c0=0, c1=T):
@@ -161,6 +161,18 @@ def tile_mix_linattn_fm_pl_relu2_kernel(tc, qc, kc, qd, st, vc_words, vc_scales,
 
         def row_close(a, r):
             mx_pass(y_bank[a, r][:], *state(a, r), "qd", 0, T, False, True)
+
+        def pair_open(a, rp, hf, number):
+            y_bank[a, rp, hf] = bank(number, "y_bank%d%d%d" % (a, rp, hf))
+            for i in range(2):
+                mx_pass(y_bank[a, rp, hf][:, i * HALF : (i + 1) * HALF], *values(a, 2 * rp + i), "h", hf * HALF, (hf + 1) * HALF, i == 0, False)
+
+        def pair_close(a, rp, hf):
+            for i in range(2):
+                mx_pass(y_bank[a, rp, hf][:, i * HALF : (i + 1) * HALF], *state(a, 2 * rp + i), "qd", hf * HALF, (hf + 1) * HALF, False, i == 1)
+
+        def relu_pair(engine, a, rp, hf):
+            engine(relu[a][:, 2 * rp : 2 * rp + 2, hf * HALF : (hf + 1) * HALF], y_bank[a, rp, hf][:].rearrange("p (r t) -> p r t", r=2))
 
         def relu_scalar(out, in_):
             nc.scalar.activation(out=out, in_=in_, func=ACT.Relu)
@@ -259,26 +271,26 @@ def tile_mix_linattn_fm_pl_relu2_kernel(tc, qc, kc, qd, st, vc_words, vc_scales,
         relu_block(relu_vector, 0, 1)
         square(0, 0, 4, 0, Q1)
         square_vector(0, 0, 4, Q1, Q2)
-        round_plain(vector, "out0", 0, Q1)
         relu_block(relu_scalar, 0, 2)
         relu_block(relu_scalar, 0, 3)
         square(0, 0, 4, Q2, Q3)
         square(0, 0, 4, Q3, T)
         store_rows(0, 0, 4)
         round_runs(vector, "st1", 0, 2)
-        deal_words(vector, 2)
+        round_plain(vector, "out0", 0, Q1)
         quantise("st1", 0, HALF)
         row_close(1, 0)
         row_close(1, 1)
-        row_open(2, 0, 4)
-        row_open(2, 1, 5)
         round_runs(vector, "st1", 2, 4)
-        round_plain(vector, "out0", Q1, Q2)
+        deal_words(vector, 2)
         quantise("st1", HALF, T)
         row_close(1, 2)
         row_close(1, 3)
+        row_open(2, 0, 4)
+        row_open(2, 1, 5)
         row_open(2, 2, 6)
         row_open(2, 3, 7)
+        round_plain(vector, "out0", Q1, Q2)
         round_plain(scalar, "out0", Q2, Q3)
         round_runs(vector, "st2", 0, 2)
         round_plain(vector, "out0", Q3, T)
@@ -312,11 +324,13 @@ def tile_mix_linattn_fm_pl_relu2_kernel(tc, qc, kc, qd, st, vc_words, vc_scales,
         square(2, 3, 4, 0, HALF)
         square(2, 3, 4, HALF, T)
         store_rows(2, 3, 4)
-        round_plain(vector, "out1")
+        round_plain(vector, "out1", 0, HALF)
+        round_plain(vector, "out1", HALF, T)
+        quantise("out1", 0, HALF)
         round_plain(scalar, "out2", 0, Q1)
         round_plain(scalar, "out2", Q3, T)
         round_plain(vector, "out2", Q1, Q2)
-        quantise("out1")
+        quantise("out1", HALF, T)
         store_codes(1)
         round_plain(vector, "out2", Q2, Q3)
         quantise("out2", 0, HALF)

@@ -217,8 +217,8 @@ def tile_mix_linattn_fm_pl_relu2_kernel(tc, qc, kc, qd, st, vc_words, vc_scales,
         load("qd", HALF, T)
         load_words(1, 2)
         load("st1")
-        load_words(2, 3)
         load("st2")
+        load_words(2, 3)
 
         deal_words(vector, 0)
         round_dealt(scalar, "kc", Q3, T)
@@ -265,44 +265,41 @@ def tile_mix_linattn_fm_pl_relu2_kernel(tc, qc, kc, qd, st, vc_words, vc_scales,
         quantise("qd", Q3, T)
         block_close(0, 3)
 
-        for r in range(PACK):
-            row_open(1, r, r)
         relu_block(relu_scalar, 0, 0)
         relu_block(relu_vector, 0, 1)
         square(0, 0, 4, 0, Q1)
         square_vector(0, 0, 4, Q1, Q2)
         relu_block(relu_scalar, 0, 2)
         relu_block(relu_scalar, 0, 3)
+        for r in range(PACK):
+            row_open(1, r, 4 + r)
         square(0, 0, 4, Q2, Q3)
         square(0, 0, 4, Q3, T)
         store_rows(0, 0, 4)
-        round_runs(vector, "st1", 0, 2)
         round_plain(vector, "out0", 0, Q1)
+        round_runs(vector, "st1", 0, 2)
+        round_plain(vector, "out0", Q1, Q2)
         quantise("st1", 0, HALF)
         row_close(1, 0)
         row_close(1, 1)
         round_runs(vector, "st1", 2, 4)
-        deal_words(vector, 2)
+        round_plain(vector, "out0", Q3, T)
         quantise("st1", HALF, T)
         row_close(1, 2)
         row_close(1, 3)
-        row_open(2, 0, 4)
-        row_open(2, 1, 5)
-        row_open(2, 2, 6)
-        row_open(2, 3, 7)
-        round_plain(vector, "out0", Q1, Q2)
         round_plain(scalar, "out0", Q2, Q3)
         round_runs(vector, "st2", 0, 2)
-        round_plain(vector, "out0", Q3, T)
+        deal_words(vector, 2)
         quantise("st2", 0, HALF)
-        row_close(2, 0)
-        row_close(2, 1)
+        for r in range(2):
+            row_open(2, r, r)
+            row_close(2, r)
         round_runs(vector, "st2", 2, 4)
-        quantise("out0", 0, HALF)
+        quantise("out0")
         quantise("st2", HALF, T)
-        row_close(2, 2)
-        row_close(2, 3)
-        quantise("out0", HALF, T)
+        for r in range(2, 4):
+            row_open(2, r, r)
+            row_close(2, r)
         relu_row(relu_scalar, 1, 0)
         relu_row(relu_scalar, 1, 1)
         square(1, 0, 1)
@@ -318,24 +315,23 @@ def tile_mix_linattn_fm_pl_relu2_kernel(tc, qc, kc, qd, st, vc_words, vc_scales,
         store_rows(1, 3, 4)
         for r in range(PACK):
             relu_row(relu_vector, 2, r)
-        for r in range(3):
+        for r in range(2):
             square(2, r, r + 1)
             store_rows(2, r, r + 1)
-        square(2, 3, 4, 0, HALF)
-        square(2, 3, 4, HALF, T)
-        store_rows(2, 3, 4)
+        square(2, 2, 4, 0, HALF)
+        square(2, 2, 4, HALF, T)
+        store_rows(2, 2, 4)
         round_plain(vector, "out1", 0, HALF)
         round_plain(vector, "out1", HALF, T)
         quantise("out1", 0, HALF)
         round_plain(scalar, "out2", 0, Q1)
-        round_plain(scalar, "out2", Q3, T)
+        round_plain(scalar, "out2", 448, T)
         round_plain(vector, "out2", Q1, Q2)
         quantise("out1", HALF, T)
         store_codes(1)
-        round_plain(vector, "out2", Q2, Q3)
+        round_plain(vector, "out2", Q2, 448)
         quantise("out2", 0, HALF)
-        store_codes(2, 0, HALF)
         quantise("out2", HALF, T)
-        store_codes(2, HALF, T)
+        store_codes(2)
         for r in range(4):
             store_scales(nc.scalar if r % 2 else nc.sync, r, 0, 3)

@@ -207,11 +207,11 @@ def tile_mix_linattn_fm_pl_relu2_kernel(tc, qc, kc, qd, st, vc_words, vc_scales,
         Q1, Q2, Q3 = P, 2 * P, 3 * P
 
         nc.vector.memset(vc_scales_raw[:].bitcast(I32), 0)
-        load_words(0, 1)
         load("kc")
         load_vc_scales()
         load("qc")
         load("dm")
+        load_words(0, 1)
         load("st0")
         load("qd", 0, HALF)
         load("qd", HALF, T)
@@ -220,7 +220,6 @@ def tile_mix_linattn_fm_pl_relu2_kernel(tc, qc, kc, qd, st, vc_words, vc_scales,
         load("st2")
         load_words(2, 3)
 
-        deal_words(vector, 0)
         round_dealt(scalar, "kc", Q3, T)
         round_dealt(vector, "kc", 0, Q3)
         deal_scales(0)
@@ -235,24 +234,27 @@ def tile_mix_linattn_fm_pl_relu2_kernel(tc, qc, kc, qd, st, vc_words, vc_scales,
         round_plain(vector, "qc", Q2, Q3)
         quantise("qc", Q1, Q2)
         h_sums(1, 1)
+
         quantise("qc", Q2, T)
         h_sums(2, 2)
         h_sums(3, 3)
+
         h_decay(0)
         h_decay(1)
         h_decay(2)
         quantise("h", 0, HALF)
         h_decay(3)
+        deal_words(scalar, 0)
         block_open(0, 0, 4)
         block_open(0, 1, 5)
-        round_dealt(scalar, "st0", 320, T)
-        round_dealt(vector, "st0", 0, 320)
+        round_dealt(scalar, "st0", 288, T)
+        round_dealt(vector, "st0", 0, 288)
         quantise("h", HALF, T)
         block_open(0, 2, 6)
         block_open(0, 3, 7)
+        round_plain(vector, "qd", 0, Q1)
+        round_plain(scalar, "qd", Q1, Q2)
         quantise("st0")
-        round_plain(scalar, "qd", 0, Q1)
-        round_plain(vector, "qd", Q1, Q2)
         quantise("qd", 0, Q1)
         block_close(0, 0)
         quantise("qd", Q1, Q2)
@@ -262,6 +264,7 @@ def tile_mix_linattn_fm_pl_relu2_kernel(tc, qc, kc, qd, st, vc_words, vc_scales,
         deal_words(vector, 1)
         quantise("qd", Q2, Q3)
         block_close(0, 2)
+
         quantise("qd", Q3, T)
         block_close(0, 3)
 
@@ -315,23 +318,24 @@ def tile_mix_linattn_fm_pl_relu2_kernel(tc, qc, kc, qd, st, vc_words, vc_scales,
         store_rows(1, 3, 4)
         for r in range(PACK):
             relu_row(relu_vector, 2, r)
-        for r in range(2):
+        for r in range(3):
             square(2, r, r + 1)
             store_rows(2, r, r + 1)
-        square(2, 2, 4, 0, HALF)
-        square(2, 2, 4, HALF, T)
-        store_rows(2, 2, 4)
+        square(2, 3, 4, 0, HALF)
+        square(2, 3, 4, HALF, T)
+        store_rows(2, 3, 4)
         round_plain(vector, "out1", 0, HALF)
         round_plain(vector, "out1", HALF, T)
         quantise("out1", 0, HALF)
         round_plain(scalar, "out2", 0, Q1)
-        round_plain(scalar, "out2", 448, T)
+        round_plain(scalar, "out2", Q3, T)
         round_plain(vector, "out2", Q1, Q2)
         quantise("out1", HALF, T)
         store_codes(1)
-        round_plain(vector, "out2", Q2, 448)
+        round_plain(vector, "out2", Q2, Q3)
         quantise("out2", 0, HALF)
+        store_codes(2, 0, HALF)
         quantise("out2", HALF, T)
-        store_codes(2)
+        store_codes(2, HALF, T)
         for r in range(4):
             store_scales(nc.scalar if r % 2 else nc.sync, r, 0, 3)

@@ -338,4 +338,4 @@ def tile_mix_linattn_fm_pl_relu2_kernel(tc, qc, kc, qd, st, vc_words, vc_scales,
         quantise("out2", HALF, T)
         store_codes(2, HALF, T)
         for r in range(4):
-            store_scales(nc.scalar if r % 2 else nc.sync, r, 0, 3)
+            store_scales(nc.sync, r, 0, 3)

@@ -98,10 +98,10 @@ def tile_mix_linattn_fm_pl_relu2_kernel(tc, qc, kc, qd, st, vc_words, vc_scales,
                 in_=source(name, c0, c1).rearrange("p j (m s r) -> p s m j r", s=2, r=2),
             )
 
-        def round_runs(copy, name, r0, r1):
+        def round_runs(copy, name, r0, r1, m0=0, m1=P):
             copy(
-                out=rounded[name][:].rearrange("p (r m j) -> p m j r", r=PACK, j=PACK)[:, :, :, r0:r1],
-                in_=source(name, 0, T).rearrange("p j (m r) -> p m j r", r=PACK)[:, :, :, r0:r1],
+                out=rounded[name][:].rearrange("p (r m j) -> p m j r", r=PACK, j=PACK)[:, m0:m1, :, r0:r1],
+                in_=source(name, 0, T).rearrange("p j (m r) -> p m j r", r=PACK)[:, m0:m1, :, r0:r1],
             )
 
         def round_plain(copy, name, c0=0, c1=T):
@@ -146,33 +146,24 @@ def tile_mix_linattn_fm_pl_relu2_kernel(tc, qc, kc, qd, st, vc_words, vc_scales,
                 op=ALU.mult,
             )
 
-        def block_open(a, tb, number):
+        def operands(kind, a, r):
+            return values(a, r) + ("h",) if kind == "values" else state(a, r) + ("qd",)
+
+        def block_open(kind, a, tb, number):
             y_bank[a, tb] = bank(number, "y_bank%d%d" % (a, tb))
             for r in range(PACK):
-                mx_pass(y_bank[a, tb][:, r * P : (r + 1) * P], *values(a, r), "h", tb * P, (tb + 1) * P, r == 0, False)
+                mx_pass(y_bank[a, tb][:, r * P : (r + 1) * P], *operands(kind, a, r), tb * P, (tb + 1) * P, r == 0, False)
 
-        def block_close(a, tb):
+        def block_close(kind, a, tb):
             for r in range(PACK):
-                mx_pass(y_bank[a, tb][:, r * P : (r + 1) * P], *state(a, r), "qd", tb * P, (tb + 1) * P, False, r == PACK - 1)
+                mx_pass(y_bank[a, tb][:, r * P : (r + 1) * P], *operands(kind, a, r), tb * P, (tb + 1) * P, False, r == PACK - 1)
 
-        def row_open(a, r, number):
+        def row_open(kind, a, r, number):
             y_bank[a, r] = bank(number, "y_bank%d%d" % (a, r))
-            mx_pass(y_bank[a, r][:], *values(a, r), "h", 0, T, True, False)
+            mx_pass(y_bank[a, r][:], *operands(kind, a, r), 0, T, True, False)
 
-        def row_close(a, r):
-            mx_pass(y_bank[a, r][:], *state(a, r), "qd", 0, T, False, True)
-
-        def pair_open(a, rp, hf, number):
-            y_bank[a, rp, hf] = bank(number, "y_bank%d%d%d" % (a, rp, hf))
-            for i in range(2):
-                mx_pass(y_bank[a, rp, hf][:, i * HALF : (i + 1) * HALF], *values(a, 2 * rp + i), "h", hf * HALF, (hf + 1) * HALF, i == 0, False)
-
-        def pair_close(a, rp, hf):
-            for i in range(2):
-                mx_pass(y_bank[a, rp, hf][:, i * HALF : (i + 1) * HALF], *state(a, 2 * rp + i), "qd", hf * HALF, (hf + 1) * HALF, False, i == 1)
-
-        def relu_pair(engine, a, rp, hf):
-            engine(relu[a][:, 2 * rp : 2 * rp + 2, hf * HALF : (hf + 1) * HALF], y_bank[a, rp, hf][:].rearrange("p (r t) -> p r t", r=2))
+        def row_close(kind, a, r):
+            mx_pass(y_bank[a, r][:], *operands(kind, a, r), 0, T, False, True)
 
         def relu_scalar(out, in_):
             nc.scalar.activation(out=out, in_=in_, func=ACT.Relu)
@@ -226,8 +217,9 @@ def tile_mix_linattn_fm_pl_relu2_kernel(tc, qc, kc, qd, st, vc_words, vc_scales,
         quantise("kc")
         deal_scales(1)
         deal_scales(2)
+        round_plain(scalar, "qc", 64, Q1)
         round_plain(scalar, "qc", Q3, T)
-        round_plain(vector, "qc", 0, Q1)
+        round_plain(vector, "qc", 0, 64)
         round_plain(vector, "qc", Q1, Q2)
         quantise("qc", 0, Q1)
         h_sums(0, 0)
@@ -245,28 +237,28 @@ def tile_mix_linattn_fm_pl_relu2_kernel(tc, qc, kc, qd, st, vc_words, vc_scales,
         quantise("h", 0, HALF)
         h_decay(3)
         deal_words(scalar, 0)
-        block_open(0, 0, 4)
-        block_open(0, 1, 5)
+        block_open("values", 0, 0, 4)
+        block_open("values", 0, 1, 5)
         round_dealt(scalar, "st0", 288, T)
         round_dealt(vector, "st0", 0, 288)
         quantise("h", HALF, T)
-        block_open(0, 2, 6)
-        block_open(0, 3, 7)
+        block_open("values", 0, 2, 6)
+        block_open("values", 0, 3, 7)
         round_plain(vector, "qd", 0, Q1)
         round_plain(scalar, "qd", Q1, Q2)
         quantise("st0")
         quantise("qd", 0, Q1)
-        block_close(0, 0)
+        block_close("state", 0, 0)
         quantise("qd", Q1, Q2)
-        block_close(0, 1)
+        block_close("state", 0, 1)
         round_plain(vector, "qd", Q2, Q3)
         round_plain(scalar, "qd", Q3, T)
         deal_words(vector, 1)
         quantise("qd", Q2, Q3)
-        block_close(0, 2)
+        block_close("state", 0, 2)
 
         quantise("qd", Q3, T)
-        block_close(0, 3)
+        block_close("state", 0, 3)
 
         relu_block(relu_scalar, 0, 0)
         relu_block(relu_vector, 0, 1)
@@ -275,7 +267,7 @@ def tile_mix_linattn_fm_pl_relu2_kernel(tc, qc, kc, qd, st, vc_words, vc_scales,
         relu_block(relu_scalar, 0, 2)
         relu_block(relu_scalar, 0, 3)
         for r in range(PACK):
-            row_open(1, r, 4 + r)
+            row_open("values", 1, r, 4 + r)
         square(0, 0, 4, Q2, Q3)
         square(0, 0, 4, Q3, T)
         store_rows(0, 0, 4)
@@ -283,26 +275,26 @@ def tile_mix_linattn_fm_pl_relu2_kernel(tc, qc, kc, qd, st, vc_words, vc_scales,
         round_runs(vector, "st1", 0, 2)
         round_plain(vector, "out0", Q1, Q2)
         quantise("st1", 0, HALF)
-        row_close(1, 0)
-        row_close(1, 1)
+        row_close("state", 1, 0)
+        row_close("state", 1, 1)
         round_runs(vector, "st1", 2, 4)
         round_plain(vector, "out0", Q3, T)
         quantise("st1", HALF, T)
-        row_close(1, 2)
-        row_close(1, 3)
+        row_close("state", 1, 2)
+        row_close("state", 1, 3)
         round_plain(scalar, "out0", Q2, Q3)
         round_runs(vector, "st2", 0, 2)
         deal_words(vector, 2)
         quantise("st2", 0, HALF)
         for r in range(2):
-            row_open(2, r, r)
-            row_close(2, r)
+            row_open("values", 2, r, r)
+            row_close("state", 2, r)
         round_runs(vector, "st2", 2, 4)
         quantise("out0")
         quantise("st2", HALF, T)
         for r in range(2, 4):
-            row_open(2, r, r)
-            row_close(2, r)
+            row_open("values", 2, r, r)
+            row_close("state", 2, r)
         relu_row(relu_scalar, 1, 0)
         relu_row(relu_scalar, 1, 1)
         square(1, 0, 1)

from contextlib import ExitStack

import concourse.mybir as mybir

K, M, T = 512, 1536, 512
FLOPS = 2 * K * T * T + 2 * T * M * T + 2 * K * M * T

F32 = mybir.dt.float32
BF16 = mybir.dt.bfloat16
U32 = mybir.dt.uint32
U16 = mybir.dt.uint16
I32 = mybir.dt.int32
U8 = mybir.dt.uint8
FP8X4 = mybir.dt.float8_e4m3fn_x4
FP4X4 = mybir.dt.float4_e2m1fn_x4
ACT = mybir.ActivationFunctionType
ALU = mybir.AluOpType

P = 128
PACK = 4
GROUP = P * PACK
GROUPS = M // GROUP
QUADRANT = 32
HALF = T // 2


def tile_mix_linattn_fm_pl_relu2_kernel(tc, qc, kc, qd, st, vc_words, vc_scales, dm, out_0, out_1, out_2):
    nc = tc.nc
    vector, scalar = nc.vector.tensor_copy, nc.scalar.copy
    with ExitStack() as ctx:
        sb = ctx.enter_context(tc.tile_pool(name="sb", bufs=1))
        psum = ctx.enter_context(tc.psum_pool(name="psum", bufs=1))
        ctx.enter_context(tc.manual_schedule())

        def tile(name, shape, dtype):
            return sb.tile(shape, dtype, name=name, align_bytes=64)

        def bank(number, name):
            return psum.tile([P, T], F32, name=name, tag="bank%d" % number)

        def four_rows(dram):
            return dram.rearrange("(p j) w -> p j w", j=PACK)

        words_raw = {}
        words = [tile("words%d" % a, [P, GROUP], U16) for a in range(GROUPS)]
        vc_scales_raw = tile("vc_scales_raw", [P, M], U8)
        vc_scales_dealt = tile("vc_scales_dealt", [P, M], U8)
        states = ["st%d" % a for a in range(GROUPS)]
        outs = ["out%d" % a for a in range(GROUPS)]
        dram = {"kc": kc, "qc": qc, "qd": qd, "dm": dm}
        for a in range(GROUPS):
            dram[states[a]] = st[:, a * GROUP : (a + 1) * GROUP]
        made = ["kc", "qc", "qd", "h"] + states
        rounded = {name: tile(name + "_bf16", [P, PACK * T], BF16) for name in made + outs}
        codes = {name: tile(name + "_codes", [P, T], U32) for name in made + outs}
        scales = {name: tile(name + "_scales", [P, T], U8)[:] for name in made}
        out_scales = tile("out_scales", [P, GROUPS, T], U8)
        relu = [tile("relu%d" % a, [P, PACK, T], F32) for a in range(GROUPS)]
        pieces = {name: [] for name in dram}
        for a in range(GROUPS):
            scales[outs[a]] = out_scales[:, a, :]
            pieces[outs[a]] = [(0, tile(outs[a] + "_f32", [P, PACK, T], F32))]
        h_bank = {}
        y_bank = {}

        def source(name, c0, c1):
            first, piece = [entry for entry in pieces[name] if entry[0] <= c0][-1]
            return piece[:, :, c0 - first : c1 - first]

        def load(name, c0=0, c1=T):
            piece = tile("%s_%d_f32" % (name, c0), [P, PACK, c1 - c0], F32)
            pieces[name].append((c0, piece))
            nc.sync.dma_start(out=piece[:], in_=four_rows(dram[name][:, c0:c1]))

        def load_words(a0, a1):
            piece = tile("words_raw%d" % a0, [P, GROUP * (a1 - a0)], U16)
            for a in range(a0, a1):
                words_raw[a] = piece[:, (a - a0) * GROUP : (a - a0 + 1) * GROUP]
            nc.sync.dma_start(out=piece[:].bitcast(I32), in_=vc_words[0][:, 2 * GROUP * a0 : 2 * GROUP * a1].bitcast(I32))

        def load_vc_scales():
            for r in range(4):
                nc.sync.dma_start(out=vc_scales_raw[r:P:QUADRANT, :].bitcast(I32), in_=vc_scales[0, r:16:4, :].bitcast(I32))

        def deal_words(copy, a):
            copy(out=words[a][:].rearrange("p (r m) -> p r m", r=PACK), in_=words_raw[a].rearrange("p (m r) -> p r m", r=PACK))

        def deal_scales(a):
            span = slice(a * GROUP, (a + 1) * GROUP)
            nc.vector.tensor_copy(
                out=vc_scales_dealt[:, span].rearrange("p (r m) -> p r m", r=PACK),
                in_=vc_scales_raw[:, span].rearrange("p (m r) -> p r m", r=PACK),
            )

        def round_dealt(copy, name, c0=0, c1=T):
            copy(
                out=rounded[name][:].rearrange("p (s r m j) -> p s m j r", s=2, r=2, j=PACK)[:, :, c0 // PACK : c1 // PACK],
                in_=source(name, c0, c1).rearrange("p j (m s r) -> p s m j r", s=2, r=2),
            )

        def round_runs(copy, name, r0, r1, m0=0, m1=P):
            copy(
                out=rounded[name][:].rearrange("p (r m j) -> p m j r", r=PACK, j=PACK)[:, m0:m1, :, r0:r1],
                in_=source(name, 0, T).rearrange("p j (m r) -> p m j r", r=PACK)[:, m0:m1, :, r0:r1],
            )

        def round_plain(copy, name, c0=0, c1=T):
            copy(
                out=rounded[name][:, PACK * c0 : PACK * c1].rearrange("p (c i j) -> p c j i", i=2, j=PACK),
                in_=source(name, c0, c1).rearrange("p j (c i) -> p c j i", i=2),
            )

        def quantise(name, c0=0, c1=T):
            nc.vector.quantize_mx(out=codes[name][:, c0:c1].bitcast(FP8X4), scales=scales[name][:, c0:c1], in_=rounded[name][:, PACK * c0 : PACK * c1])

        def mx_pass(out, stationary, stationary_scale, name, c0, c1, start, stop):
            nc.tensor.matmul_mx(
                out=out,
                lhsT=stationary,
                lhsT_scale=stationary_scale,
                rhs=codes[name][:, c0:c1].bitcast(FP8X4),
                rhs_scale=scales[name][:, c0:c1],
                start=start,
                stop=stop,
            )

        def values(a, r):
            col = a * GROUP + r * P
            return words[a][:, r * P : (r + 1) * P].bitcast(U8).bitcast(FP4X4), vc_scales_dealt[:, col : col + P]

        def state(a, r):
            run = slice(r * P, (r + 1) * P)
            return codes[states[a]][:, run].bitcast(FP8X4), scales[states[a]][:, run]

        def h_sums(tb, number):
            h_bank[tb] = bank(number, "h_bank%d" % tb)
            for r in range(PACK):
                run = slice(r * P, (r + 1) * P)
                mx_pass(h_bank[tb][:, run], codes["kc"][:, run].bitcast(FP8X4), scales["kc"][:, run], "qc", tb * P, (tb + 1) * P, True, True)

        def h_decay(tb):
            nc.vector.tensor_tensor(
                out=rounded["h"][:, GROUP * tb : GROUP * (tb + 1)].rearrange("p (c i r) -> p c r i", i=2, r=PACK),
                in0=h_bank[tb][:].rearrange("p (r c i) -> p c r i", r=PACK, i=2),
                in1=source("dm", tb * P, (tb + 1) * P).rearrange("p r (c i) -> p c r i", i=2),
                op=ALU.mult,
            )

        def operands(kind, a, r):
            return values(a, r) + ("h",) if kind == "values" else state(a, r) + ("qd",)

        def block_open(kind, a, tb, number):
            y_bank[a, tb] = bank(number, "y_bank%d%d" % (a, tb))
            for r in range(PACK):
                mx_pass(y_bank[a, tb][:, r * P : (r + 1) * P], *operands(kind, a, r), tb * P, (tb + 1) * P, r == 0, False)

        def block_close(kind, a, tb):
            for r in range(PACK):
                mx_pass(y_bank[a, tb][:, r * P : (r + 1) * P], *operands(kind, a, r), tb * P, (tb + 1) * P, False, r == PACK - 1)

        def row_open(kind, a, r, number):
            y_bank[a, r] = bank(number, "y_bank%d%d" % (a, r))
            mx_pass(y_bank[a, r][:], *operands(kind, a, r), 0, T, True, False)

        def row_close(kind, a, r):
            mx_pass(y_bank[a, r][:], *operands(kind, a, r), 0, T, False, True)

        def relu_scalar(out, in_):
            nc.scalar.activation(out=out, in_=in_, func=ACT.Relu)

        def relu_vector(out, in_):
            nc.vector.tensor_scalar(out=out, in0=in_, scalar1=0.0, scalar2=None, op0=ALU.max)

        def relu_block(engine, a, tb):
            engine(relu[a][:, :, tb * P : (tb + 1) * P], y_bank[a, tb][:].rearrange("p (r t) -> p r t", r=PACK))

        def relu_row(engine, a, r):
            engine(relu[a][:, r, :], y_bank[a, r][:])

        def square(a, r0, r1, c0=0, c1=T):
            nc.scalar.activation(out=source(outs[a], 0, T)[:, r0:r1, c0:c1], in_=relu[a][:, r0:r1, c0:c1], func=ACT.Square)

        def square_vector(a, r0, r1, c0=0, c1=T):
            nc.vector.tensor_tensor(out=source(outs[a], 0, T)[:, r0:r1, c0:c1], in0=relu[a][:, r0:r1, c0:c1], in1=relu[a][:, r0:r1, c0:c1], op=ALU.mult)

        def store_rows(a, r0, r1, c0=0, c1=T):
            nc.sync.dma_start(out=four_rows(out_0[a * GROUP : (a + 1) * GROUP, c0:c1])[:, r0:r1, :], in_=source(outs[a], 0, T)[:, r0:r1, c0:c1])

        def store_codes(a, c0=0, c1=T):
            nc.sync.dma_start(out=out_1[a].rearrange("p t i -> p (t i)").bitcast(I32)[:, c0:c1], in_=codes[outs[a]][:, c0:c1].bitcast(I32))

        def store_scales(queue, r, a0, a1):
            queue.dma_start(
                out=out_2.rearrange("a q t -> q a t")[r:16:4, a0:a1].bitcast(I32),
                in_=out_scales[r:P:QUADRANT, a0:a1].bitcast(I32),
            )

        Q1, Q2, Q3 = P, 2 * P, 3 * P

        nc.vector.memset(vc_scales_raw[:].bitcast(I32), 0)
        load("kc")
        load_vc_scales()
        load("qc")
        load("dm")
        load_words(0, 1)
        load("st0")
        load("qd", 0, HALF)
        load("qd", HALF, T)
        load_words(1, 2)
        load("st1")
        load("st2")
        load_words(2, 3)

        round_dealt(scalar, "kc", Q3, T)
        round_dealt(vector, "kc", 0, Q3)
        deal_scales(0)
        quantise("kc")
        deal_scales(1)
        deal_scales(2)
        round_plain(scalar, "qc", 64, Q1)
        round_plain(scalar, "qc", Q3, T)
        round_plain(vector, "qc", 0, 64)
        round_plain(vector, "qc", Q1, Q2)
        quantise("qc", 0, Q1)
        h_sums(0, 0)
        round_plain(vector, "qc", Q2, Q3)
        quantise("qc", Q1, Q2)
        h_sums(1, 1)

        quantise("qc", Q2, T)
        h_sums(2, 2)
        h_sums(3, 3)

        h_decay(0)
        h_decay(1)
        h_decay(2)
        quantise("h", 0, HALF)
        h_decay(3)
        deal_words(scalar, 0)
        block_open("values", 0, 0, 4)
        block_open("values", 0, 1, 5)
        round_dealt(scalar, "st0", 288, T)
        round_dealt(vector, "st0", 0, 288)
        quantise("h", HALF, T)
        block_open("values", 0, 2, 6)
        block_open("values", 0, 3, 7)
        round_plain(vector, "qd", 0, Q1)
        round_plain(scalar, "qd", Q1, Q2)
        quantise("st0")
        quantise("qd", 0, Q1)
        block_close("state", 0, 0)
        quantise("qd", Q1, Q2)
        block_close("state", 0, 1)
        round_plain(vector, "qd", Q2, Q3)
        round_plain(scalar, "qd", Q3, T)
        deal_words(vector, 1)
        quantise("qd", Q2, Q3)
        block_close("state", 0, 2)

        quantise("qd", Q3, T)
        block_close("state", 0, 3)

        relu_block(relu_scalar, 0, 0)
        relu_block(relu_vector, 0, 1)
        square(0, 0, 4, 0, Q1)
        square_vector(0, 0, 4, Q1, Q2)
        relu_block(relu_scalar, 0, 2)
        relu_block(relu_scalar, 0, 3)
        for r in range(PACK):
            row_open("values", 1, r, 4 + r)
        square(0, 0, 4, Q2, Q3)
        square(0, 0, 4, Q3, T)
        store_rows(0, 0, 4)
        round_plain(vector, "out0", 0, Q1)
        round_runs(vector, "st1", 0, 2)
        round_plain(vector, "out0", Q1, Q2)
        quantise("st1", 0, HALF)
        row_close("state", 1, 0)
        row_close("state", 1, 1)
        round_runs(vector, "st1", 2, 4)
        round_plain(vector, "out0", Q3, T)
        quantise("st1", HALF, T)
        row_close("state", 1, 2)
        row_close("state", 1, 3)
        round_plain(scalar, "out0", Q2, Q3)
        round_runs(vector, "st2", 0, 2)
        deal_words(vector, 2)
        quantise("st2", 0, HALF)
        for r in range(2):
            row_open("values", 2, r, r)
            row_close("state", 2, r)
        round_runs(vector, "st2", 2, 4)
        quantise("out0")
        quantise("st2", HALF, T)
        for r in range(2, 4):
            row_open("values", 2, r, r)
            row_close("state", 2, r)
        relu_row(relu_scalar, 1, 0)
        relu_row(relu_scalar, 1, 1)
        square(1, 0, 1)
        store_rows(1, 0, 1)
        square(1, 1, 2)
        store_rows(1, 1, 2)
        store_codes(0)
        relu_row(relu_scalar, 1, 2)
        relu_row(relu_scalar, 1, 3)
        square(1, 2, 3)
        store_rows(1, 2, 3)
        square(1, 3, 4)
        store_rows(1, 3, 4)
        for r in range(PACK):
            relu_row(relu_vector, 2, r)
        for r in range(3):
            square(2, r, r + 1)
            store_rows(2, r, r + 1)
        square(2, 3, 4, 0, HALF)
        square(2, 3, 4, HALF, T)
        store_rows(2, 3, 4)
        round_plain(vector, "out1", 0, HALF)
        round_plain(vector, "out1", HALF, T)
        quantise("out1", 0, HALF)
        round_plain(scalar, "out2", 0, Q1)
        round_plain(scalar, "out2", Q3, T)
        round_plain(vector, "out2", Q1, Q2)
        quantise("out1", HALF, T)
        store_codes(1)
        round_plain(vector, "out2", Q2, Q3)
        quantise("out2", 0, HALF)
        store_codes(2, 0, HALF)
        quantise("out2", HALF, T)
        store_codes(2, HALF, T)
        for r in range(4):
            store_scales(nc.sync, r, 0, 3)
